import numpy as np, ml_dtypes
CORES = [3,11,19,27,35,43,51,59]
N = 8
BF = ml_dtypes.bfloat16
def gentries(a):
    return np.ascontiguousarray(a.reshape(8, 16, -1).transpose(0, 2, 1)).reshape(8, -1)
def gtable(e):
    e = np.asarray(e); return np.ascontiguousarray(e.reshape(8, -1, 16).transpose(0, 2, 1)).reshape(128, -1).astype(np.int32)
V, G, H, Q, ST = 2048, 1024, 2, 2, 4
W = V + H * G
def come(v, snd):
    return np.concatenate([np.take_along_axis(np.roll(v, -d, axis=0), np.roll(snd[:, :, d - 1], -d, axis=0), 2) for d in range(1, H + 1)], axis=2)
def some(rng):
    return np.ascontiguousarray(np.argsort(rng.random((N, 8, H, V)), axis=-1)[..., :G])
def traffic(rng):
    snd = some(rng); pace = rng.permutation(np.array([2, 3, 4, 4, 6, 8, 8, 16])).reshape(1, 8, 1)
    base = 64 + (rng.random((N, 8, V)) * W * pace).astype(np.int64)
    lane = (rng.random((N, 8, V)) < 0.3 + 0.4 * rng.random((1, 8, 1))).astype(np.int64)
    pw = np.concatenate([base, come(base, snd)], axis=2); lw = np.concatenate([lane, come(lane, snd)], axis=2)
    la = np.zeros((N, 8, V), np.int64); lb = np.zeros((N, 8, V), np.int64)
    for q in range(N):
        for g in range(8):
            order = np.argsort(pw[q, g], kind="stable"); l = lw[q, g][order]; two = []
            for c in (0, 1):
                m = order[l == c]; i = np.searchsorted(pw[q, g][m], base[q, g], side="right"); two.append(m[np.minimum(i, len(m) - 1)])
            la[q, g] = np.where(lane[q, g] == 0, two[0], two[1]); lb[q, g] = np.where(lane[q, g] == 0, two[1], two[0])
    return jitter(rng, base), la, lb, snd
def jitter(rng, base):
    off = rng.integers(0, 2 ** 19, (1, 8, 16, 1)); size = rng.choice(np.array([1.0, 2.0, 4.0]), (N, 8, 1, 1))
    return np.clip(base[:, :, None, :] + off + np.rint(rng.standard_normal((N, 8, 16, V)) * size).astype(np.int64), 0, 2 ** 20 - 1)
def stray(rng, ptr, share):
    return np.where(rng.random(ptr.shape) < share, rng.integers(0, W, ptr.shape), ptr)
def pack(x, la, lb, snd):
    return {"x0": np.ascontiguousarray(x.reshape(N, 128, V)).astype(np.int32), "la": la.astype(np.int32), "lb": lb.astype(np.int32),
            "snd": np.stack([gtable(s.reshape(8, -1)) for s in snd])}
def setup_inputs(rng):
    x, la, lb, snd = traffic(rng)
    return pack(x, stray(rng, la, 0.1), stray(rng, lb, 0.1), snd)
def setup_inputs_ties(rng):
    snd = some(rng); x = np.zeros((N, 8, 16, V), np.int64); la = np.zeros((N, 8, V), np.int64); lb = np.zeros((N, 8, V), np.int64); h = V // 2
    for q in range(N):
        for g in range(8):
            o = rng.permutation(V); fa, fb, fo = o[0:h:2], o[1:h:2], o[h:]; n = h // 2
            xa = rng.integers(2 ** 10, 2 ** 19, (16, n)); cnt = rng.choice(np.array([0, 8, 9, 10, 16]), n)
            xb = xa + 4 + (np.argsort(rng.random((16, n)), axis=0) < cnt)
            i = rng.integers(0, n, V - h); c = rng.choice(np.array([0, 0, 7, 8, 9, 16]), V - h)
            e = np.where(c == 0, rng.integers(1, 15, (16, V - h)), (np.argsort(rng.random((16, V - h)), axis=0) >= c).astype(np.int64))
            x[q, g][:, fa] = xa; x[q, g][:, fb] = xb; x[q, g][:, fo] = xb[:, i] - e
            la[q, g] = np.arange(V); lb[q, g] = np.arange(V)
            la[q, g, fo] = stray(rng, fa[i], 0.125); lb[q, g, fo] = stray(rng, fb[i], 0.125)
    return pack(x, la, lb, snd)
def setup_inputs_weave(rng):
    snd = some(rng); base = 64 + rng.integers(0, 2 ** 15, (N, 8, V)); pw = np.concatenate([base, come(base, snd)], axis=2)
    la = np.zeros((N, 8, V), np.int64); lb = np.zeros((N, 8, V), np.int64)
    for q in range(N):
        for g in range(8):
            order = np.argsort(pw[q, g], kind="stable"); cand = order if g % 4 < 2 else order[(order < V) & (order % Q == 0)]; n = len(cand)
            la[q, g] = cand[rng.integers(0, n, V)]; hi = cand[rng.integers(2 * n // 3, n, V)]; lo = cand[rng.integers(0, n // 3, V)]
            lb[q, g] = hi if g % 2 == 0 else np.where(rng.random(V) < 0.5, hi, lo)
    return pack(jitter(rng, base), la, lb, snd)
def setup_inputs_alike(rng):
    x, la, lb, snd = traffic(rng)
    snd[:, ::2] = rng.choice(np.array([0, 3, V // 2, V - 1]), (N, 4, H, G))
    ends = np.array([0, V - 1, V, W - 1])
    la[:, 1] = rng.choice(ends, (N, V)); lb[:, 1] = rng.choice(ends, (N, V))
    la[:, 2] = rng.integers(V, W, (N, V)); lb[:, 2] = rng.integers(V, W, (N, V))
    la[:, 3] = rng.integers(0, V, (N, V)); lb[:, 3] = la[:, 3]
    lb[:, 4] = np.arange(V)
    x[:, 5] = rng.integers(0, 2 ** 20, (1, 16, 1))
    la[:, 6] = rng.choice(ends)
    return pack(x, la, lb, snd)
def setup_inputs_crowd(rng):
    snd = some(rng); x = rng.integers(0, 2 ** 20, (N, 8, 16, V)); la = rng.integers(0, W, (N, 8, V)); lb = rng.integers(0, W, (N, 8, V)); v = np.arange(V)
    for q in range(N):
        for g in range(8):
            kind = (q + g) % 4; tu = rng.permutation(v[v % Q == 0]); nt = rng.permutation(v[v % Q != 0]); xx = x[q, g]
            if kind == 0:
                hi, lo = nt[:64], nt[64:128]
                xx[:] = rng.integers(2 ** 17, 2 ** 18, (16, V)); xx[:, lo] = rng.integers(0, 2 ** 16, (16, 64)); xx[:, hi] = rng.integers(2 ** 19, 2 ** 20, (16, 64))
                la[q, g] = rng.choice(lo, V); lb[q, g] = rng.choice(hi, V)
            elif kind == 1:
                one, top = tu[0], nt[:8]
                xx[:] = rng.integers(2 ** 17, 2 ** 18, (16, V)); xx[:, nt[8:10]] = rng.integers(0, 2 ** 16, (16, 2))
                xx[:, one] = rng.integers(2 ** 19, 3 * 2 ** 18, 16); xx[:, top] = rng.integers(3 * 2 ** 18, 2 ** 20, (16, 8))
                la[q, g] = np.where(v % Q == 0, rng.choice(top, V), nt[8]); lb[q, g] = one
                la[q, g, one] = nt[9]; lb[q, g, one] = top[0]
            elif kind == 2:
                o = rng.permutation(V); n = V // 4; fa, fb, fo = o[:n], o[n:2 * n], o[2 * n:]; i = rng.integers(0, n, V - 2 * n)
                far = np.argsort(rng.random((16, 1)), axis=0) < 8
                xa = np.exp2(17 * rng.random((16, n))).astype(np.int64)
                xx[:, fa] = xa; xx[:, fb] = np.where(far, xa + rng.integers(5, 21, (16, n)), rng.integers(3 * 2 ** 18, 2 ** 20, (16, n)))
                xx[:, fo] = np.where(far, 2 ** 20 - np.exp2(18 * rng.random((16, V - 2 * n))).astype(np.int64), rng.integers(2 ** 18, 2 ** 19, (16, V - 2 * n)))
                la[q, g] = v; lb[q, g] = v; la[q, g, fo] = fa[i]; lb[q, g, fo] = fb[i]
    return pack(x, la, lb, snd)
def setup_inputs_spread(rng):
    snd = some(rng)
    x = np.minimum((np.exp2(20 * rng.random((N, 8, 1, V))) * rng.random((N, 8, 16, V))).astype(np.int64), 2 ** 20 - 1)
    end = rng.random((N, 8, 1, V)); x = np.where(end < 0.02, 0, np.where(end > 0.98, 2 ** 20 - 1, x))
    up = rng.choice(np.array([1.0, 1.5, 3.0]), (N, 8, 1)); dn = rng.choice(np.array([1.0, 1.5, 3.0]), (N, 8, 1))
    la = np.minimum((rng.random((N, 8, V)) ** up * W).astype(np.int64), W - 1); lb = W - 1 - np.minimum((rng.random((N, 8, V)) ** dn * W).astype(np.int64), W - 1)
    return pack(x, la, lb, snd)
def check_inputs(d):
    bad = []
    for k, hi in (("x0", 2 ** 20 - 1), ("la", W - 1), ("lb", W - 1), ("snd", V - 1)):
        if np.min(d[k]) < 0 or np.max(d[k]) > hi: bad.append("range of " + k)
    return bad
def reference(x0, la, lb, snd):
    x = x0.astype(np.int64).reshape(N, 8, 16, V); a = la.astype(np.int64); b = lb.astype(np.int64)
    sl = np.stack([gentries(s) for s in snd]).astype(np.int64).reshape(N, 8, H, G)
    turn = np.arange(V) % Q
    own = np.zeros((N, 8, H * G), np.int64) + np.arange(V, W)
    never = np.zeros((N, 8, H * G), bool)
    for t in range(ST):
        w = [x]
        for d in range(1, H + 1):
            q = (np.arange(N) + d) % N
            w.append(np.take_along_axis(x[q], sl[q][:, :, d - 1][:, :, None, :], 3))
        w = np.concatenate(w, axis=3)
        ga = np.take_along_axis(w, a[:, :, None, :], 3) - x; gb = np.take_along_axis(w, b[:, :, None, :], 3) - x
        gone = np.add.reduce((gb <= 0).astype(np.int64), axis=2) >= 9
        ch = (np.add.reduce((gb > ga + 4).astype(np.int64), axis=2) >= 9) & ~gone & (turn == t % Q)
        x = x + np.minimum(np.maximum(ga - 2, 0), 5)
        aw = np.concatenate([a, own], axis=2); cw = np.concatenate([ch, never], axis=2)
        aa = np.take_along_axis(aw, a, 2); ab = np.take_along_axis(aw, b, 2)
        ca = np.take_along_axis(cw, a, 2); cb = np.take_along_axis(cw, b, 2)
        na = np.where(ch | (cb & ~gone), b, np.where(ca, aa, a))
        nb = np.where(ch, a, np.where(gone | cb, ab, b))
        a, b = na, nb
    return {"yx": x.reshape(N, 128, V).astype(np.float32), "ya": a.astype(np.float32), "yb": b.astype(np.float32)}

@@ -1,0 +1,474 @@
+from concourse.bass import DstId, RemoteDMATransfer
+from concourse.mybir import AluOpType as ALU, AxisListType, ActivationFunctionType as ACT
+
+N, V, G, ST, K = 8, 2048, 1024, 4, 4096
+HELP = 256
+SPLIT = 8
+
+SCRATCH = {}
+for dt_, bufs in (("float32", dict(W=2 * V, Y=V, YX=V, S0=V, HB=2 * HELP, WA4=G, TF=256, M=256, COL=144, PF=16, IF=128, RM=16, RM2=8, WR=48, WT=48, WK=4)),
+                  ("bfloat16", dict(S1=V, S2=V, S3=V, L1=V, L2=V, L3=V, GA=V, D=V, MP=V, MC=G, P=2 * V, GP=2 * V, HI=256, LO=256, FL=192, GHI=128, Z=256,
+                                    GLO=128, IB=128, BC=144, BX=256, PM=512, WA=144, WC=144, UN=16 * 128, SI=6 * 128, ZER=512, ONE=64, BIT=512)),
+                  ("int32", dict(X0=V, SNI=128, TN=256, AB=256, TG=256, PI=8, GLI=128, GLJ=128)), ("uint16", dict(SN=128, OFF=256))):
+    for name_, n_ in bufs.items():
+        SCRATCH[name_] = ("sbuf", [128, n_], dt_)
+SCRATCH.update({"E0": ("sbuf", [128, 16, 16], "int32"), "E1": ("sbuf", [128, 16, 32], "float32"), "E2": ("sbuf", [128, 16, 32], "float32")})
+for name_, n_ in (("GH", 2048), ("STG", 1024), ("PCD", 512), ("PAB", 512)):
+    SCRATCH[name_] = ("psum", [128, n_], "float32")
+SEMAPHORES = (["cv", "ca", "cp", "cg", "dx", "dsn", "dl", "dy", "dc0", "dc1", "dc2", "dc3", "ls", "h0", "h1"]
+              + ["ar%d_%d" % (t, d) for t in range(ST) for d in (1, 2)])
+
+
+def helpers(T, topo, r):
+    c = T.cores[r]
+    out = {}
+    for d in (1, 2):
+        dst = T.cores[(r - d) % N]
+        out[d] = [h for h in topo.cores_of(c) if topo.die(h) != topo.die(c) and topo.may_write(h, dst)
+                  and T.rank_of(h) is None and h not in out.values()][0]
+    return out
+
+
+def spare(topo, src, helper, dst, d):
+    e = [x for x in topo.engines(src, helper) if x not in topo.engines(src, dst)]
+    return e[(d - 1) * len(e) // 2:d * len(e) // 2]
+
+
+def helper_program(g, core, T, topo, r, d):
+    dst = T.cores[(r - d) % N]
+    rid, pid, _ = topo.addr(dst)
+    for j in range(2):
+        g.wait_ge(T.sem["h%d" % j], len(spare(topo, T.cores[r], core, dst, d)))
+        c0 = V + (d - 1) * G + j * HELP
+        g.remote_dma(T.W[:, c0:c0 + HELP], T.HB[:, j * HELP:(j + 1) * HELP], T.sem["ar0_%d" % d], T.sem.ls, pid, rid, topo.mask(core, dst))
+    g.wait_ge(T.sem.ls, 2 * len(topo.engines(core, dst)))
+
+
+def rank_program(g, core, T, topo):
+    rank = T.rank_of(core)
+    if rank is None:
+        for r in range(N):
+            for d, h in helpers(T, topo, r).items():
+                if h == core:
+                    helper_program(g, core, T, topo, r, d)
+        return
+    q = {"v": g.vector, "a": g.scalar, "p": g.tensor, "g": g, "s": g.sync}
+    cnt = {"v": 0, "a": 0, "p": 0, "g": 0}
+    seen = {e: {} for e in q}
+    wrote, read, total = {}, {}, {"ls": 0}
+
+    def wait(e, tok):
+        if seen[e].get(tok[0], 0) < tok[1]:
+            q[e].wait_ge(T.sem[tok[0]], tok[1])
+            seen[e][tok[0]] = tok[1]
+
+    def order(e, r, w, x, late=False):
+        own = "c" + e
+        need = {}
+        toks = [wrote[k] for k in r if k in wrote and not (e == "p" and wrote[k][0] == own)]
+        for k in list(w) + list(x):
+            toks += read.get(k, []) + ([wrote[k]] if k in wrote and (late or wrote[k][0] != own) else [])
+        for s, v in toks:
+            need[s] = max(need.get(s, 0), v)
+        for s in need:
+            wait(e, (s, need[s]))
+
+    def note(tok, r, w, x):
+        for k in list(w) + list(x):
+            wrote[k] = tok
+            read[k] = []
+        for k in r:
+            if k not in w:
+                read.setdefault(k, []).append(tok)
+
+    def op(e, fn, args, r=(), w=(), x=(), **kw):
+        order(e, r, w, x)
+        cnt[e] += 1
+        fn(*args, **kw).then_inc(T.sem["c" + e], 1)
+        note(("c" + e, cnt[e]), r, w, x)
+
+    def mm(lst, r, x):
+        order("p", r, (), x)
+        for a in lst[:-1]:
+            g.tensor.matmul(*a)
+        cnt["p"] += 1
+        g.tensor.matmul(*lst[-1]).then_inc(T.sem.cp, 1)
+        note(("cp", cnt["p"]), r, (), x)
+
+    def dma(e, out, in_, sem, r=(), w=()):
+        order(e, r, w, (), True)
+        q[e].dma_start(out, in_).then_inc(T.sem[sem], 16)
+        total[sem] = total.get(sem, 0) + 16
+        note((sem, total[sem]), r, w, ())
+
+    def ts(o, i, s1, o0, s2=None, o1=None, **k):
+        op("v", g.vector.tensor_scalar, (o, i, s1, None, o0) if o1 is None else (o, i, s1, s2, o0, o1), **k)
+
+    def tt(o, a, b, alu, **k):
+        op("v", g.vector.tensor_tensor, (o, a, b, alu), **k)
+
+    def cp(o, i, **k):
+        op("v", g.vector.tensor_copy, (o, i), **k)
+
+    def fill(o, c, key):
+        op("v", g.vector.memset, (o, float(c)), w=[key])
+
+    def act(o, i, f, **k):
+        op("a", g.scalar.activation, (o, i, f), **k)
+
+    dsts = {d: T.cores[(rank - d) % N] for d in (1, 2)}
+
+    def send(d, out, in_, sem, r):
+        order("g", r, (), ())
+        rid, pid, _ = topo.addr(dsts[d])
+        g.remote_dma(out, in_, T.sem[sem], T.sem.ls, pid, rid, topo.mask(core, dsts[d]))
+        total["ls"] += len(topo.engines(core, dsts[d]))
+
+    dma("s", T.X0[:], T.x0[:], "dx", w=["X0"])
+    dma("a", T.SNI[:], T.snd[:], "dsn", w=["SNI"])
+    dma("a", T.TN[:, 0:128], T.la[:], "dl")
+    dma("a", T.TN[:, 128:256], T.lb[:], "dl", w=["TN"])
+    for d in (1, 2):
+        src = (rank + d) % N
+        n1 = len(topo.engines(T.cores[src], core))
+        total["ar0_%d" % d] = n1 + 2 * len(topo.engines(helpers(T, topo, src)[d], core))
+        wrote["Wg%d" % d] = ("ar0_%d" % d, total["ar0_%d" % d])
+        for t in range(1, ST):
+            total["ar%d_%d" % (t, d)] = n1
+            wrote["L%d_%d" % (t, d)] = ("ar%d_%d" % (t, d), n1)
+
+    op("g", g.iota, (T.PI[:, 0:1], [[0, 1]], 0, 1), w=["PI0"])
+    op("g", g.iota, (T.COL[:], [[1, 144]], 0, 0), w=["COL"], allow_small_or_imprecise_dtypes=True)
+    op("g", g.iota, (T.GHI[:], [[0, 2], [32, 64]], V, 0), w=["GHI"], allow_small_or_imprecise_dtypes=True)
+    op("g", g.iota, (T.GLI[:], [[1, 2], [0, 64]], 0, 2), w=["GLI"])
+    wa = [1, 1, 2 * K, -16 * K, -8, -K]
+    wc = [0, 0, 17 * K, -136 * K, 0, -K]
+    bias = [0, 8, -8, -8, 1, 1]
+    fill(T.WR[:], 0, "WR")
+    fill(T.ONE[:], 1, "ONE")
+    wait("v", wrote["WR"])
+    for j, row in enumerate((wa, wc, bias)):
+        for c in range(6):
+            if row[c]:
+                fill(T.WR[:, 16 * j + c:16 * j + c + 1], row[c], "WR")
+    ts(T.PI[:, 1:2], T.PI[:, 0:1], 15, ALU.bitwise_and, r=["PI0"], w=["PI"])
+    ts(T.PI[:, 2:3], T.PI[:, 0:1], 112, ALU.bitwise_and, r=["PI0"], w=["PI"])
+    ts(T.PI[:, 3:4], T.PI[:, 0:1], 4, ALU.logical_shift_right, 1, ALU.bitwise_and, r=["PI0"], w=["PI"])
+    ts(T.PI[:, 4:5], T.PI[:, 0:1], 1, ALU.bitwise_and, r=["PI0"], w=["PI"])
+    cp(T.PF[:, 0:5], T.PI[:, 0:5], r=["PI0", "PI"], w=["PF"])
+    ts(T.BC[:], T.COL[:], -16.0, ALU.add, T.PF[:, 2:3], ALU.is_equal, r=["COL", "PF"], w=["BC"])
+    ts(T.RM[:], T.COL[:, 0:16], T.PF[:, 1:2], ALU.is_equal, r=["COL", "PF"], w=["RM"])
+    for j, (m, c) in enumerate(((1.0, 2), (-1.0, 2), (-1000.0, 0), (1000.0, 0))):
+        ts(T.PF[:, 8 + j:9 + j], T.PF[:, 4:5], m, ALU.mult, T.PF[:, c:c + 1], ALU.add, r=["PF"], w=["PG"])
+    tt(T.RM2[:], T.RM[:, 0::2], T.RM[:, 1::2], ALU.add, r=["RM"], w=["RM2"])
+    for e in range(2):
+        ts(T.BX[:, 128 * e:128 * (e + 1)], T.COL[:, 0:128], -1.0 * e, ALU.add, T.PF[:, 8 + e:9 + e], ALU.is_equal, r=["COL", "PG"], w=["BX"])
+    ts(T.PF[:, 5:6], T.PF[:, 3:4], -1.0, ALU.mult, 1.0, ALU.add, r=["PF"], w=["PF5"])
+    ts(T.GLJ[:], T.GLI[:], 31, ALU.bitwise_and, r=["GLI"], w=["GLJ"])
+    for j in range(3):
+        tt(T.WT[:, 16 * j:16 * j + 16], T.WR[:, 16 * j:16 * j + 16], T.RM[:], ALU.mult, r=["WR", "RM"], w=["WT"])
+    cp(T.GLO[:], T.GLJ[:], r=["GLJ"], w=["GLO"])
+    for j in range(3):
+        op("v", g.vector.tensor_reduce, (T.WK[:, j:j + 1], T.WT[:, 16 * j:16 * j + 16], AxisListType.X, ALU.add), r=["WT"], w=["WK"])
+    ts(T.IB[:], T.COL[:, 0:128], T.PF[:, 0:1], ALU.is_equal, r=["COL", "PF"], w=["IB"])
+    for j, c in enumerate((0.0, -1.0, 1000.0, 1001.0)):
+        ts(T.PM[:, 128 * j:128 * (j + 1)], T.COL[:, 0:128], c, ALU.add, T.PF[:, 10 + j // 2:11 + j // 2], ALU.is_equal, r=["COL", "PG"], w=["PM"])
+    cp(T.SN[:], T.SNI[:], r=["SNI"], w=["SN"])
+
+    def bc(i, mat=T.BC):
+        return mat[:, 16 - i:144 - i]
+
+    def un(i):
+        return T.UN[:, 128 * i:128 * (i + 1)]
+
+    for i in range(16):
+        act(un(i), T.BX[:, 128 * (i % 2):128 * (i % 2 + 1)], ACT.Identity, scale=T.RM2[:, i // 2:i // 2 + 1], r=["BX", "RM2"], w=["UN"])
+    si = {s: T.SI[:, 128 * j:128 * (j + 1)] for j, s in enumerate([136 * K, -1296 * K, 1152 * K, 24 * K, -24 * K, -K])}
+    for s in si:
+        act(si[s], T.IB[:], ACT.Identity, scale=float(s), r=["IB"], w=["SI"])
+
+    side = {0: T.PF[:, 5:6], 1: T.PF[:, 3:4]}
+    for p in range(2):
+        for s in range(2):
+            ts(T.E1[:, 8 * p:8 * p + 8, 16 * s:16 * s + 16], T.TN[:, p::2], side[s], ALU.mult, r=["TN", "PF", "PF5"], w=["E1"])
+
+    def first(d, a, b):
+        c0 = (d - 1) * G
+        cp(T.S0[:, c0 + a:c0 + b], T.X0[:].indirect(T.SN[:, (c0 + a) // 16:(c0 + b) // 16]), r=["X0", "SN"], w=["S0_%d_%d" % (d, a)])
+        return "S0_%d_%d" % (d, a)
+
+    hs = helpers(T, topo, rank)
+    for j in range(2):
+        order("g", [first(d, j * HELP, (j + 1) * HELP) for d in (1, 2)], (), ())
+        trs = []
+        for d in (1, 2):
+            part = spare(topo, core, hs[d], dsts[d], d)
+            rid, pid, _ = topo.addr(hs[d])
+            c0 = (d - 1) * G + j * HELP
+            trs.append(RemoteDMATransfer(dst_ids=[DstId(rid=rid, pnc=pid)], dma_engine_mask=sum(1 << e for e in part), remote_sem=T.sem["h%d" % j],
+                                         src=T.S0[:, c0:c0 + HELP], dst=T.HB[:, j * HELP:(j + 1) * HELP]))
+            total["ls"] += len(part)
+        g.remote_dma_fused(trs, local_sem=T.sem.ls)
+        c0 = j * G
+        send(j + 1, T.W[:, V + c0 + 2 * HELP:V + c0 + G], T.S0[:, c0 + 2 * HELP:c0 + G], "ar0_%d" % (j + 1), [first(j + 1, 2 * HELP, G)])
+
+    op("v", g.vector.transpose, (T.E2[:], T.E1[:]), r=["E1"], w=["E2"])
+    fill(T.ZER[:], 0, "ZER")
+    for b in range(4):
+        tt(T.AB[:, b::4], T.E2[:, b::4, 0:16], T.E2[:, b::4, 16:32], ALU.add, r=["E2"], w=["AB"])
+    ts(T.IF[:], T.COL[:, 0:128], T.PF[:, 0:1], ALU.is_equal, r=["COL", "PF"], w=["IF"])
+    cp(T.OFF[:], T.AB[:], r=["AB"], w=["OFF"])
+
+    def bank(key, i=0, step=1):
+        c0 = 512 * int(key[-1])
+        return T[key[:-1]][:, c0 + i:c0 + 512:step]
+
+    def pair(hi, lo, r):
+        lst = []
+        for e in range(2):
+            for p in range(2):
+                o = T.PAB[:, 128 * e + 64 * p:128 * e + 64 * p + 64]
+                lst += [(o, T.PM[:, 256 * e:256 * e + 128], hi(p), True, False), (o, T.PM[:, 256 * e + 128:256 * e + 256], lo(p), False, True)]
+        mm(lst, ["PM"] + r, ["PAB0"])
+        act(T.Z[:], T.PAB[:, 0:256], ACT.Copy, w=["Z"], x=["PAB0"])
+
+    def spread(key, c0, opened):
+        return [(bank(key, i, 16), un(i), T.Z[:, 128 * (i % 2) + c0:128 * (i % 2) + c0 + 32], not opened, not opened) for i in range(16)]
+
+    def evac(key, h, p, ghost=0):
+        act(T.P[:, V * ghost + G * h + p:V * ghost + G * (h + 1):2], bank(key), ACT.Relu, bias=T.WK[:, 2:3], r=["WK"], w=["P%d%d%d" % (ghost, p, h)], x=[key])
+
+    pair(lambda p: T.GHI[:, 64 * p:64 * p + 64], lambda p: T.GLO[:, 64 * p:64 * p + 64], ["GHI", "GLO"])
+    for p in range(2):
+        for h in range(2):
+            key = "GH%d" % (2 * p + h)
+            mm(spread(key, 64 * p + 32 * h, False), ["UN", "Z"], [key])
+            evac(key, h, p, 1)
+    allp = ["P%d%d%d" % (a, b, c) for a in range(2) for b in range(2) for c in range(2)] + ["OFF"]
+    own = ["W%d" % k for k in range(4)]
+    ys = ["Y%d" % k for k in range(4)]
+    allw = own + ["Wg1", "Wg2", "OFF"]
+
+    def piece(buf, arr, p, a=0, b=64):
+        return buf[:, 128 * p + 64 * arr + a:128 * p + 64 * arr + b]
+
+    def wrap(out, mat, src, c0, first_):
+        return [(out, bc(i, mat), src[:, c0 + i:c0 + G:16], first_ and i == 0, i == 15) for i in range(16)]
+
+    for t in range(ST):
+        pa, pi, last = t % 2, 1 - t % 2, t == ST - 1
+        Yc = T.Y if t else T.X0
+        stages = ["GH2", "GH3", "GH0", "GH1"] if last else ["PAB0", "STG0", "STG1", "STG0"]
+        want = T.FL[:, 128:192]
+
+        def at(arr, p):
+            return T.W[:].indirect(piece(T.OFF, arr, p))
+
+        def lead():
+            act(T.WA4[:], at(0, pa), ACT.Identity, bias=4.0, r=allw, w=["WA4"])
+
+        def gap(p):
+            tt(T.GA[:, p::2], at(0, p), Yc[:, p::2], ALU.subtract, r=allw + ys, w=["GA%d" % p])
+
+        def clip():
+            ts(T.D[:], T.GA[:], 2.0, ALU.max, 7.0, ALU.min, r=["GA0", "GA1"], w=["D"])
+
+        def passing(p):
+            tt(T.MP[:, G * p:G * (p + 1)], at(1, p), Yc[:, p::2], ALU.is_le, r=allw + ys, w=["MP%d" % p])
+
+        def own_votes(p):
+            mm(wrap(T.PCD[:, 256 + 64 * p:320 + 64 * p], T.BC, T.MP, G * p, True), ["BC", "MP%d" % p], ["PCD0"])
+
+        def marks():
+            passing(pa)
+            for h in range(2):
+                key = "STG%d" % h
+                lst = [(bank(key), bc(3), T.MP[:, G * pa + 512 * h:G * pa + 512 * (h + 1)], last, False)]
+                mm(lst + (spread(key, 64 * pa + 32 * h, True) if last else []), ["BC", "UN", "Z", "MP%d" % pa], [key])
+            if not last:
+                own_votes(pa)
+            tt(T.MC[:], at(1, pa), T.WA4[:], ALU.is_gt, r=allw + ["WA4"], w=["MC"])
+            for h in range(2):
+                key = "STG%d" % h
+                mm([(bank(key), bc(2), T.MC[:, 512 * h:512 * (h + 1)], False, True)], ["BC", "MC"], [key])
+                evac(key, h, pa)
+            if last:
+                own_votes(pa)
+            mm(wrap(T.PCD[:, 384:448], T.BC, T.MC, 0, True), ["BC", "MC"], ["PCD0"])
+
+        def flags():
+            ts(T.FL[:], T.PCD[:, 256:448], 8.5, ALU.is_ge, w=["FL"], x=["PCD0"])
+
+        def stage(k):
+            mm([(bank(stages[k]), T.IB[:], T.D[:, 512 * k:512 * (k + 1)], not last, True)], ["IB", "D"], [stages[k]])
+
+        def move(k):
+            cols = slice(512 * k, 512 * (k + 1))
+            if last:
+                tt(T.YX[:, cols], bank(stages[k]), Yc[:, cols], ALU.add, r=[ys[k]], w=["YX%d" % k], x=[stages[k]])
+                dma("s", T.yx[:, cols], T.YX[:, cols], "dy", r=["YX%d" % k])
+            else:
+                tt(T.Y[:, cols], bank(stages[k]), Yc[:, cols], ALU.add, r=[ys[k]], w=[ys[k]], x=[stages[k]])
+                dma("s", T.W[:, cols], T.Y[:, cols], "dc%d" % k, r=[ys[k]], w=[own[k]])
+
+        def look(e, arr, p, a=0, b=64):
+            c0 = G * (2 * p + arr)
+            o, src = T.GP[:, c0 + 16 * a:c0 + 16 * b], T.P[:].indirect(piece(T.OFF, arr, p, a, b))
+            if e == "a":
+                act(o, src, ACT.Copy, r=allp, w=gp(arr, p))
+            else:
+                cp(o, src, r=allp, w=gp(arr, p)[:1] if b < 64 else gp(arr, p))
+
+        def gp(arr, p):
+            return ["GP%d%dv" % (arr, p), "GP%d%da" % (arr, p)]
+
+        def gone(p):
+            return T.FL[:, 64 * p:64 * p + 64]
+
+        def whole(o, arr, p):
+            return [(o, T.IB[:], piece(T.HI, arr, p), True, False), (o, T.IB[:], piece(T.LO, arr, p), False, False)]
+
+        def cand_d(p):
+            o = piece(T.PCD, 1, p)
+            lst = [(o, si[24 * K], want, False, False), (o, si[-24 * K], gone(p), False, False)] if p == pa else []
+            mm(whole(o, 0, p) + lst + [(o, si[-K], T.ONE[:], False, True)], ["IB", "SI", "HI", "LO", "FL", "ONE"], ["PCD0"])
+
+        def cand_c(p):
+            o = piece(T.PCD, 0, p)
+            lst = [(o, si[-1296 * K], gone(p), False, False)] + ([(o, si[1152 * K], want, False, False)] if p == pa else [])
+            mm(whole(o, 1, p) + lst + wrap(o, T.WC, T.GP, G * (2 * p + 1), False), ["IB", "SI", "HI", "LO", "FL", "WC"] + gp(1, p), ["PCD0"])
+
+        def cand_b(p):
+            o = piece(T.PAB, 1, p)
+            mm([(o, si[136 * K], gone(p), True, False)] + wrap(o, T.WA, T.GP, G * (2 * p + 1), False), ["SI", "FL", "WA"] + gp(1, p), ["PAB0"])
+
+        def cand_a(p):
+            mm(wrap(piece(T.PAB, 0, p), T.WA, T.GP, G * 2 * p, True), ["WA"] + gp(0, p), ["PAB0"])
+
+        def ghost_open(k):
+            mm([(bank("GH%d" % k), T.IF[:], T.W[:, V + 512 * k:V + 512 * (k + 1)], True, False)], ["IF", "Wg%d" % (1 + k // 2)], ["GH%d" % k])
+
+        def ghost_add(d):
+            for k in (2 * d - 2, 2 * d - 1):
+                mm([(bank("GH%d" % k), T.IB[:], T["L%d" % (t + 1)][:, 512 * k:512 * (k + 1)], False, True)], ["IB", "L%d_%d" % (t + 1, d)], ["GH%d" % k])
+
+        def ghost_out(d):
+            c0 = (d - 1) * G
+            act(T.W[:, V + c0:V + c0 + G], T.GH[:, c0:c0 + G], ACT.Copy, w=["Wg%d" % d], x=["GH%d" % (2 * d - 2), "GH%d" % (2 * d - 1)])
+
+        def best():
+            tt(T.M[:], T.PCD[:, 0:256], T.AB[:], ALU.max, r=["AB"], w=["M"], x=["PCD0"])
+
+        cp(T.HI[:], T.AB[:], r=["AB"], w=["HI"])
+        tt(T.LO[:], T.AB[:], T.HI[:], ALU.subtract, r=["AB", "HI"], w=["LO"])
+        if t == 0:
+            cp(T.W[:, 0:V], T.X0[:], r=["X0"], w=own)
+            ts(T.WA[:], T.BC[:], T.WK[:, 0:1], ALU.mult, r=["BC", "WK"], w=["WA"])
+            ts(T.WC[:], T.BC[:], T.WK[:, 1:2], ALU.mult, r=["BC", "WK"], w=["WC"])
+            fill(T.BIT[:], 2.0 * ST / K, "BIT")
+        elif last:
+            lead()
+        else:
+            ghost_open(0)
+            ghost_open(1)
+        pair(lambda p: piece(T.HI, 0, p), lambda p: piece(T.LO, 0, p), ["HI", "LO"])
+        if t and not last:
+            lead()
+            ghost_open(2)
+        for h in range(2):
+            key = ("GH%d" if last else "STG%d") % h
+            mm(spread(key, 64 * pi + 32 * h, False), ["UN", "Z"], [key])
+            evac(key, h, pi)
+        if not last:
+            if t:
+                ghost_open(3)
+            for h in range(2):
+                key = "STG%d" % h
+                mm([(bank(key), T.IB[:], T.ZER[:], True, False)] + spread(key, 64 * pa + 32 * h, True), ["UN", "Z", "IB", "ZER"], [key])
+            if t == 0:
+                lead()
+                for k in range(4):
+                    ghost_open(k)
+            gap(0)
+            gap(1)
+            clip()
+            for d in (1, 2):
+                cols = slice((d - 1) * G, d * G)
+                sb, key = T["S%d" % (t + 1)][:, cols], "S%d_%d" % (t + 1, d)
+                act(sb, T.D[:].indirect(T.SN[:, (d - 1) * 64:d * 64]), ACT.Copy, r=["D", "SN"], w=[key])
+                send(d, T["L%d" % (t + 1)][:, cols], sb, "ar%d_%d" % (t + 1, d), [key])
+            stage(0)
+            marks()
+            passing(pi)
+            stage(1)
+            stage(2)
+            own_votes(pi)
+            look("a", 1, 0)
+            look("a", 1, 1)
+            move(0)
+            move(1)
+            stage(3)
+            flags()
+            move(2)
+            move(3)
+            look("v", 0, 1)
+            order("v", (), gp(0, 0), ())
+            look("a", 0, 0, SPLIT, 64)
+            del wrote[gp(0, 0)[0]]
+            look("v", 0, 0, 0, SPLIT)
+            cand_d(0)
+            cand_d(1)
+            cand_c(0)
+            cand_b(0)
+            ghost_add(1)
+            cand_c(1)
+            cand_b(1)
+            best()
+            cand_a(1)
+            cand_a(0)
+            ghost_add(2)
+            ghost_out(1)
+            ghost_out(2)
+        else:
+            marks()
+            for arr, p in ((1, 0), (1, 1), (0, 0), (0, 1)):
+                look("a", arr, p)
+            passing(pi)
+            own_votes(pi)
+            gap(0)
+            flags()
+            gap(1)
+            clip()
+            for key in stages:
+                mm([(bank(key), si[-K], T.BIT[:], True, False)], ["SI", "BIT"], [key])
+            cand_d(0)
+            cand_d(1)
+            cand_c(0)
+            cand_b(0)
+            for k in range(4):
+                stage(k)
+            cand_c(1)
+            cand_b(1)
+            for k in range(4):
+                move(k)
+            best()
+            cand_a(0)
+            cand_a(1)
+        tt(T.TG[:], T.PAB[:, 0:256], T.M[:], ALU.max, r=["M"], w=["TG"], x=["PAB0"])
+        if not last:
+            ts(T.AB[:], T.TG[:], K - 1, ALU.bitwise_and, r=["TG"], w=["AB"])
+            cp(T.OFF[:], T.AB[:], r=["AB"], w=["OFF"])
+
+    for b in range(4):
+        ts(T.E0[:, b::4, :], T.TG[:, b::4], K - 1, ALU.bitwise_and, r=["TG"], w=["E0"])
+    for s in range(2):
+        ts(T.E1[:, :, 16 * s:16 * s + 16], T.E0[:], side[s], ALU.mult, r=["E0", "PF", "PF5"], w=["E1"])
+    op("v", g.vector.transpose, (T.E2[:], T.E1[:]), r=["E1"], w=["E2"])
+    for p in range(2):
+        tt(T.TF[:, p::2], T.E2[:, 8 * p:8 * p + 8, 0:16], T.E2[:, 8 * p:8 * p + 8, 16:32], ALU.add, r=["E2"], w=["TF"])
+    dma("s", T.ya[:], T.TF[:, 0:128], "dy", r=["TF"])
+    dma("a", T.yb[:], T.TF[:, 128:256], "dy", r=["TF"])
+    for e in cnt:
+        wait("g", ("c" + e, cnt[e]))
+    for s in total:
+        wait("g", (s, total[s]))

@@ -2,20 +2,24 @@ from concourse.bass import DstId, RemoteDMATransfer
 from concourse.mybir import AluOpType as ALU, AxisListType, ActivationFunctionType as ACT
 
 N, V, G, ST, K = 8, 2048, 1024, 4, 4096
-HELP = 256
+PC = 256
 SPLIT = 8
+SPLITL = 0
+SENDV = 0
+OPEN = (0, 2)
 
 SCRATCH = {}
-for dt_, bufs in (("float32", dict(W=2 * V, Y=V, YX=V, S0=V, HB=2 * HELP, WA4=G, TF=256, M=256, COL=144, PF=16, IF=128, RM=16, RM2=8, WR=48, WT=48, WK=4)),
-                  ("bfloat16", dict(S1=V, S2=V, S3=V, L1=V, L2=V, L3=V, GA=V, D=V, MP=V, MC=G, P=2 * V, GP=2 * V, HI=256, LO=256, FL=192, GHI=128, Z=256,
-                                    GLO=128, IB=128, BC=144, BX=256, PM=512, WA=144, WC=144, UN=16 * 128, SI=6 * 128, ZER=512, ONE=64, BIT=512)),
+for dt_, bufs in (("float32", dict(W=2 * V, Y0=V, Y1=V, S0=V, HB=2 * PC, WA4=G, TF=256, M=256, ABF=256, ABT=256, GF=128, PMF=256, COL=144, PF=16,
+                                   IF=128, RM=16, RM2=8, WR=64, WT=64, WK=8)),
+                  ("bfloat16", dict(S1=V, S2=V, S3=V, L1=V, L2=V, L3=V, GA=V, D=V, MP=V, MC=G, P=2 * V, GP=2 * V, HI=256, FL=192, CB=128, GHI=128, Z=512,
+                                    IB=128, BC=144, BX=128, PM=256, PMH=256, WA=144, WE=144, WF=144, UN=8 + 8 * 128, SI=4 * 128, ONE=256)),
                   ("int32", dict(X0=V, SNI=128, TN=256, AB=256, TG=256, PI=8, GLI=128, GLJ=128)), ("uint16", dict(SN=128, OFF=256))):
     for name_, n_ in bufs.items():
         SCRATCH[name_] = ("sbuf", [128, n_], dt_)
-SCRATCH.update({"E0": ("sbuf", [128, 16, 16], "int32"), "E1": ("sbuf", [128, 16, 32], "float32"), "E2": ("sbuf", [128, 16, 32], "float32")})
-for name_, n_ in (("GH", 2048), ("STG", 1024), ("PCD", 512), ("PAB", 512)):
+SCRATCH.update({"E1": ("sbuf", [128, 16, 32], "float32"), "E2": ("sbuf", [128, 16, 32], "float32")})
+for name_, n_ in (("GH", 2048), ("STG", 1024), ("C", 1024)):
     SCRATCH[name_] = ("psum", [128, n_], "float32")
-SEMAPHORES = (["cv", "ca", "cp", "cg", "dx", "dsn", "dl", "dy", "dc0", "dc1", "dc2", "dc3", "ls", "h0", "h1"]
+SEMAPHORES = (["cv", "ca", "cp", "cg", "dx", "dsn", "dl", "dy", "ls", "h0", "h1", "dc0", "dc1", "dc2", "dc3"]
               + ["ar%d_%d" % (t, d) for t in range(ST) for d in (1, 2)])
 
 
@@ -39,8 +43,8 @@ def helper_program(g, core, T, topo, r, d):
     rid, pid, _ = topo.addr(dst)
     for j in range(2):
         g.wait_ge(T.sem["h%d" % j], len(spare(topo, T.cores[r], core, dst, d)))
-        c0 = V + (d - 1) * G + j * HELP
-        g.remote_dma(T.W[:, c0:c0 + HELP], T.HB[:, j * HELP:(j + 1) * HELP], T.sem["ar0_%d" % d], T.sem.ls, pid, rid, topo.mask(core, dst))
+        c0 = V + (d - 1) * G + j * PC
+        g.remote_dma(T.W[:, c0:c0 + PC], T.HB[:, j * PC:(j + 1) * PC], T.sem["ar0_%d" % d], T.sem.ls, pid, rid, topo.mask(core, dst))
     g.wait_ge(T.sem.ls, 2 * len(topo.engines(core, dst)))
 
 
@@ -116,6 +120,12 @@ def rank_program(g, core, T, topo):
     def act(o, i, f, **k):
         op("a", g.scalar.activation, (o, i, f), **k)
 
+    def copy(e, o, i, **k):
+        if e == "a":
+            act(o, i, ACT.Copy, **k)
+        else:
+            cp(o, i, **k)
+
     dsts = {d: T.cores[(rank - d) % N] for d in (1, 2)}
 
     def send(d, out, in_, sem, r):
@@ -128,11 +138,13 @@ def rank_program(g, core, T, topo):
     dma("a", T.SNI[:], T.snd[:], "dsn", w=["SNI"])
     dma("a", T.TN[:, 0:128], T.la[:], "dl")
     dma("a", T.TN[:, 128:256], T.lb[:], "dl", w=["TN"])
+    gk = ["Wg%d" % k for k in range(4)]
     for d in (1, 2):
         src = (rank + d) % N
         n1 = len(topo.engines(T.cores[src], core))
         total["ar0_%d" % d] = n1 + 2 * len(topo.engines(helpers(T, topo, src)[d], core))
-        wrote["Wg%d" % d] = ("ar0_%d" % d, total["ar0_%d" % d])
+        for k in (2 * d - 2, 2 * d - 1):
+            wrote[gk[k]] = ("ar0_%d" % d, total["ar0_%d" % d])
         for t in range(1, ST):
             total["ar%d_%d" % (t, d)] = n1
             wrote["L%d_%d" % (t, d)] = ("ar%d_%d" % (t, d), n1)
@@ -141,183 +153,227 @@ def rank_program(g, core, T, topo):
     op("g", g.iota, (T.COL[:], [[1, 144]], 0, 0), w=["COL"], allow_small_or_imprecise_dtypes=True)
     op("g", g.iota, (T.GHI[:], [[0, 2], [32, 64]], V, 0), w=["GHI"], allow_small_or_imprecise_dtypes=True)
     op("g", g.iota, (T.GLI[:], [[1, 2], [0, 64]], 0, 2), w=["GLI"])
-    wa = [1, 1, 2 * K, -16 * K, -8, -K]
-    wc = [0, 0, 17 * K, -136 * K, 0, -K]
-    bias = [0, 8, -8, -8, 1, 1]
+    wa = [1, 1, 2 * K, -16 * K, -8, -K, 0, 0]
+    bias = [0, 8, -8, -8, 1, 1, 0, 8]
+    we = [1, 1, 0, 0, -8, 0, 0, 0]
+    wf = [0, 0, 0, 0, -8, 0, 1, 1]
     fill(T.WR[:], 0, "WR")
     fill(T.ONE[:], 1, "ONE")
+    fill(T.UN[:, 0:8], 0, "UN")
+    for j, (sh, m) in enumerate(((0, 15), (0, 112), (4, 1), (0, 1), (0, 7), (3, 1))):
+        ts(T.PI[:, 1 + j:2 + j], T.PI[:, 0:1], sh, ALU.logical_shift_right, m, ALU.bitwise_and, r=["PI0"], w=["PI"])
     wait("v", wrote["WR"])
-    for j, row in enumerate((wa, wc, bias)):
-        for c in range(6):
+    rows = (wa, we, bias, wf)
+    for j, row in enumerate(rows[:2]):
+        for c in range(8):
             if row[c]:
                 fill(T.WR[:, 16 * j + c:16 * j + c + 1], row[c], "WR")
-    ts(T.PI[:, 1:2], T.PI[:, 0:1], 15, ALU.bitwise_and, r=["PI0"], w=["PI"])
-    ts(T.PI[:, 2:3], T.PI[:, 0:1], 112, ALU.bitwise_and, r=["PI0"], w=["PI"])
-    ts(T.PI[:, 3:4], T.PI[:, 0:1], 4, ALU.logical_shift_right, 1, ALU.bitwise_and, r=["PI0"], w=["PI"])
-    ts(T.PI[:, 4:5], T.PI[:, 0:1], 1, ALU.bitwise_and, r=["PI0"], w=["PI"])
-    cp(T.PF[:, 0:5], T.PI[:, 0:5], r=["PI0", "PI"], w=["PF"])
-    ts(T.BC[:], T.COL[:], -16.0, ALU.add, T.PF[:, 2:3], ALU.is_equal, r=["COL", "PF"], w=["BC"])
+    cp(T.PF[:, 0:7], T.PI[:, 0:7], r=["PI0", "PI"], w=["PF"])
+    for j, row in enumerate(rows[2:], 2):
+        for c in range(8):
+            if row[c]:
+                fill(T.WR[:, 16 * j + c:16 * j + c + 1], row[c], "WR")
     ts(T.RM[:], T.COL[:, 0:16], T.PF[:, 1:2], ALU.is_equal, r=["COL", "PF"], w=["RM"])
-    for j, (m, c) in enumerate(((1.0, 2), (-1.0, 2), (-1000.0, 0), (1000.0, 0))):
-        ts(T.PF[:, 8 + j:9 + j], T.PF[:, 4:5], m, ALU.mult, T.PF[:, c:c + 1], ALU.add, r=["PF"], w=["PG"])
-    tt(T.RM2[:], T.RM[:, 0::2], T.RM[:, 1::2], ALU.add, r=["RM"], w=["RM2"])
-    for e in range(2):
-        ts(T.BX[:, 128 * e:128 * (e + 1)], T.COL[:, 0:128], -1.0 * e, ALU.add, T.PF[:, 8 + e:9 + e], ALU.is_equal, r=["COL", "PG"], w=["BX"])
-    ts(T.PF[:, 5:6], T.PF[:, 3:4], -1.0, ALU.mult, 1.0, ALU.add, r=["PF"], w=["PF5"])
-    ts(T.GLJ[:], T.GLI[:], 31, ALU.bitwise_and, r=["GLI"], w=["GLJ"])
-    for j in range(3):
-        tt(T.WT[:, 16 * j:16 * j + 16], T.WR[:, 16 * j:16 * j + 16], T.RM[:], ALU.mult, r=["WR", "RM"], w=["WT"])
-    cp(T.GLO[:], T.GLJ[:], r=["GLJ"], w=["GLO"])
-    for j in range(3):
-        op("v", g.vector.tensor_reduce, (T.WK[:, j:j + 1], T.WT[:, 16 * j:16 * j + 16], AxisListType.X, ALU.add), r=["WT"], w=["WK"])
+    ts(T.PF[:, 8:9], T.PF[:, 4:5], T.PF[:, 2:3], ALU.add, r=["PF"], w=["PG"])
+    ts(T.PF[:, 9:10], T.PF[:, 5:6], 2.0, ALU.mult, T.PF[:, 2:3], ALU.add, r=["PF"], w=["PG"])
     ts(T.IB[:], T.COL[:, 0:128], T.PF[:, 0:1], ALU.is_equal, r=["COL", "PF"], w=["IB"])
-    for j, c in enumerate((0.0, -1.0, 1000.0, 1001.0)):
-        ts(T.PM[:, 128 * j:128 * (j + 1)], T.COL[:, 0:128], c, ALU.add, T.PF[:, 10 + j // 2:11 + j // 2], ALU.is_equal, r=["COL", "PG"], w=["PM"])
+    ts(T.BC[:], T.COL[:], -16.0, ALU.add, T.PF[:, 2:3], ALU.is_equal, r=["COL", "PF"], w=["BC"])
     cp(T.SN[:], T.SNI[:], r=["SNI"], w=["SN"])
+    tt(T.RM2[:], T.RM[:, 0::2], T.RM[:, 1::2], ALU.add, r=["RM"], w=["RM2"])
+    ts(T.BX[:], T.COL[:, 0:128], T.PF[:, 8:9], ALU.is_equal, r=["COL", "PG"], w=["BX"])
+    ts(T.PF[:, 10:11], T.PF[:, 6:7], 1000.0, ALU.mult, T.PF[:, 9:10], ALU.add, r=["PF", "PG"], w=["PH"])
+    ts(T.PF[:, 7:8], T.PF[:, 3:4], -1.0, ALU.mult, 1.0, ALU.add, r=["PF"], w=["PF7"])
+    ts(T.GLJ[:], T.GLI[:], 31, ALU.bitwise_and, r=["GLI"], w=["GLJ"])
+    for j in range(len(rows)):
+        tt(T.WT[:, 16 * j:16 * j + 16], T.WR[:, 16 * j:16 * j + 16], T.RM[:], ALU.mult, r=["WR", "RM"], w=["WT"])
 
     def bc(i, mat=T.BC):
         return mat[:, 16 - i:144 - i]
 
-    def un(i):
-        return T.UN[:, 128 * i:128 * (i + 1)]
+    def un(i, arr=0):
+        return T.UN[:, 8 + 128 * i - 6 * arr:136 + 128 * i - 6 * arr]
 
-    for i in range(16):
-        act(un(i), T.BX[:, 128 * (i % 2):128 * (i % 2 + 1)], ACT.Identity, scale=T.RM2[:, i // 2:i // 2 + 1], r=["BX", "RM2"], w=["UN"])
-    si = {s: T.SI[:, 128 * j:128 * (j + 1)] for j, s in enumerate([136 * K, -1296 * K, 1152 * K, 24 * K, -24 * K, -K])}
+    for i in range(8):
+        act(un(i), T.BX[:], ACT.Identity, scale=T.RM2[:, i:i + 1], r=["BX", "RM2"], w=["UN"])
+    si = {s: T.SI[:, 128 * j:128 * (j + 1)] for j, s in enumerate([136 * K, 24 * K, -72 * K, -K])}
     for s in si:
         act(si[s], T.IB[:], ACT.Identity, scale=float(s), r=["IB"], w=["SI"])
+    act(T.IF[:], T.IB[:], ACT.Copy, r=["IB"], w=["IF"])
 
-    side = {0: T.PF[:, 5:6], 1: T.PF[:, 3:4]}
-    for p in range(2):
-        for s in range(2):
-            ts(T.E1[:, 8 * p:8 * p + 8, 16 * s:16 * s + 16], T.TN[:, p::2], side[s], ALU.mult, r=["TN", "PF", "PF5"], w=["E1"])
+    hs = helpers(T, topo, rank)
 
     def first(d, a, b):
         c0 = (d - 1) * G
-        cp(T.S0[:, c0 + a:c0 + b], T.X0[:].indirect(T.SN[:, (c0 + a) // 16:(c0 + b) // 16]), r=["X0", "SN"], w=["S0_%d_%d" % (d, a)])
+        ts(T.S0[:, c0 + a:c0 + b], T.X0[:].indirect(T.SN[:, (c0 + a) // 16:(c0 + b) // 16]), -2.0 * ST, ALU.add, r=["X0", "SN"], w=["S0_%d_%d" % (d, a)])
         return "S0_%d_%d" % (d, a)
 
-    hs = helpers(T, topo, rank)
     for j in range(2):
-        order("g", [first(d, j * HELP, (j + 1) * HELP) for d in (1, 2)], (), ())
+        order("g", [first(d, j * PC, (j + 1) * PC) for d in (1, 2)], (), ())
         trs = []
         for d in (1, 2):
             part = spare(topo, core, hs[d], dsts[d], d)
             rid, pid, _ = topo.addr(hs[d])
-            c0 = (d - 1) * G + j * HELP
+            c0 = (d - 1) * G + j * PC
             trs.append(RemoteDMATransfer(dst_ids=[DstId(rid=rid, pnc=pid)], dma_engine_mask=sum(1 << e for e in part), remote_sem=T.sem["h%d" % j],
-                                         src=T.S0[:, c0:c0 + HELP], dst=T.HB[:, j * HELP:(j + 1) * HELP]))
+                                         src=T.S0[:, c0:c0 + PC], dst=T.HB[:, j * PC:(j + 1) * PC]))
             total["ls"] += len(part)
         g.remote_dma_fused(trs, local_sem=T.sem.ls)
         c0 = j * G
-        send(j + 1, T.W[:, V + c0 + 2 * HELP:V + c0 + G], T.S0[:, c0 + 2 * HELP:c0 + G], "ar0_%d" % (j + 1), [first(j + 1, 2 * HELP, G)])
+        send(j + 1, T.W[:, V + c0 + 2 * PC:V + c0 + G], T.S0[:, c0 + 2 * PC:c0 + G], "ar0_%d" % (j + 1), [first(j + 1, 2 * PC, G)])
 
+    for s in range(2):
+        cols = slice(128 * s, 128 * (s + 1))
+        ts(T.PM[:, cols], T.COL[:, 0:128], 1000.0 * s, ALU.add, T.PF[:, 10:11], ALU.is_equal, r=["COL", "PH"], w=["PM"])
+        ts(T.PMF[:, cols], T.COL[:, 0:128], 1000.0 * s - 1.0, ALU.add, T.PF[:, 10:11], ALU.is_equal, r=["COL", "PH"], w=["PMF"])
+    tt(T.GF[:], T.GLJ[:], T.GHI[:], ALU.add, r=["GLJ", "GHI"], w=["GF"])
+    for j in range(len(rows)):
+        op("v", g.vector.tensor_reduce, (T.WK[:, j:j + 1], T.WT[:, 16 * j:16 * j + 16], AxisListType.X, ALU.add), r=["WT"], w=["WK"])
+    tt(T.PMH[:], T.PM[:], T.PMF[:], ALU.subtract, r=["PM", "PMF"], w=["PMH"])
+    side = {0: T.PF[:, 7:8], 1: T.PF[:, 3:4]}
+    for arr in range(2):
+        for p in range(2):
+            for s in range(2):
+                ts(T.E1[:, 8 * arr + 4 * p:8 * arr + 4 * p + 4, 16 * s:16 * s + 16], T.TN[:, 128 * arr + p:128 * (arr + 1):2], side[s], ALU.mult,
+                   r=["TN", "PF", "PF7"], w=["E1"])
+    for j, mat in ((0, T.WA), (1, T.WE), (3, T.WF)):
+        ts(mat[:], T.BC[:], T.WK[:, j:j + 1], ALU.mult, r=["BC", "WK"], w=["WM"])
     op("v", g.vector.transpose, (T.E2[:], T.E1[:]), r=["E1"], w=["E2"])
-    fill(T.ZER[:], 0, "ZER")
+    own = ["W%d" % k for k in range(4)]
+    yk = [["Y%d%d" % (j, k) for k in range(4)] for j in range(2)]
     for b in range(4):
-        tt(T.AB[:, b::4], T.E2[:, b::4, 0:16], T.E2[:, b::4, 16:32], ALU.add, r=["E2"], w=["AB"])
-    ts(T.IF[:], T.COL[:, 0:128], T.PF[:, 0:1], ALU.is_equal, r=["COL", "PF"], w=["IF"])
-    cp(T.OFF[:], T.AB[:], r=["AB"], w=["OFF"])
+        tt(T.ABF[:, b::4], T.E2[:, b::4, 0:16], T.E2[:, b::4, 16:32], ALU.add, r=["E2"], w=["ABF0", "ABF1"])
+    ts(T.W[:, 0:V], T.X0[:], -2.0 * ST, ALU.add, r=["X0"], w=own)
+    cp(T.OFF[:], T.ABF[:], r=["ABF0", "ABF1"], w=["OFF0", "OFF1"])
+    ts(T.Y0[:], T.X0[:], -2.0 * ST, ALU.add, r=["X0"], w=yk[0])
 
     def bank(key, i=0, step=1):
         c0 = 512 * int(key[-1])
         return T[key[:-1]][:, c0 + i:c0 + 512:step]
 
-    def pair(hi, lo, r):
+    def pair(hi, whole_, r):
         lst = []
-        for e in range(2):
-            for p in range(2):
-                o = T.PAB[:, 128 * e + 64 * p:128 * e + 64 * p + 64]
-                lst += [(o, T.PM[:, 256 * e:256 * e + 128], hi(p), True, False), (o, T.PM[:, 256 * e + 128:256 * e + 256], lo(p), False, True)]
-        mm(lst, ["PM"] + r, ["PAB0"])
-        act(T.Z[:], T.PAB[:, 0:256], ACT.Copy, w=["Z"], x=["PAB0"])
+        for p in range(2):
+            for s in range(2):
+                o = T.C[:, 256 + 128 * p + s:384 + 128 * p:2]
+                lst += [(o, T.PMH[:, 128 * s:128 * s + 128], hi(p), True, False), (o, T.PMF[:, 128 * s:128 * s + 128], whole_(p), False, True)]
+        mm(lst, ["PMH", "PMF"] + r, ["C0"])
 
-    def spread(key, c0, opened):
-        return [(bank(key, i, 16), un(i), T.Z[:, 128 * (i % 2) + c0:128 * (i % 2) + c0 + 32], not opened, not opened) for i in range(16)]
+    def zed(arr=0):
+        act(T.Z[:, 256 * arr:256 * (arr + 1)], T.C[:, 256:512], ACT.Copy, w=["Z%d" % arr], x=["C0"])
+
+    def spread(key, p, h, start, stop, arr=0):
+        c0 = 256 * arr + 128 * p + 64 * h
+        mm([(bank(key, i, 8), un(i, arr), T.Z[:, c0:c0 + 64], start and i == 0, stop and i == 7) for i in range(8)], ["UN", "Z%d" % arr], [key])
 
     def evac(key, h, p, ghost=0):
         act(T.P[:, V * ghost + G * h + p:V * ghost + G * (h + 1):2], bank(key), ACT.Relu, bias=T.WK[:, 2:3], r=["WK"], w=["P%d%d%d" % (ghost, p, h)], x=[key])
 
-    pair(lambda p: T.GHI[:, 64 * p:64 * p + 64], lambda p: T.GLO[:, 64 * p:64 * p + 64], ["GHI", "GLO"])
+    pair(lambda p: T.GHI[:, 64 * p:64 * p + 64], lambda p: T.GF[:, 64 * p:64 * p + 64], ["GHI", "GF"])
+    zed()
     for p in range(2):
         for h in range(2):
             key = "GH%d" % (2 * p + h)
-            mm(spread(key, 64 * p + 32 * h, False), ["UN", "Z"], [key])
+            spread(key, p, h, True, True)
             evac(key, h, p, 1)
-    allp = ["P%d%d%d" % (a, b, c) for a in range(2) for b in range(2) for c in range(2)] + ["OFF"]
-    own = ["W%d" % k for k in range(4)]
-    ys = ["Y%d" % k for k in range(4)]
-    allw = own + ["Wg1", "Wg2", "OFF"]
+    allp = ["P%d%d%d" % (a, b, c) for a in range(2) for b in range(2) for c in range(2)]
+    allw = own + gk
+    free = ["GH%d" % k for k in range(4) if k not in OPEN]
 
     def piece(buf, arr, p, a=0, b=64):
-        return buf[:, 128 * p + 64 * arr + a:128 * p + 64 * arr + b]
+        return buf[:, 128 * arr + 64 * p + a:128 * arr + 64 * p + b]
 
-    def wrap(out, mat, src, c0, first_):
-        return [(out, bc(i, mat), src[:, c0 + i:c0 + G:16], first_ and i == 0, i == 15) for i in range(16)]
+    def side_(buf, arr):
+        return buf[:, 128 * arr:128 * (arr + 1)]
+
+    def high(arr):
+        act(side_(T.HI, arr), side_(T.ABF, arr), ACT.Copy, r=["ABF%d" % arr], w=["HI%d" % arr])
+
+    def pieces(arr):
+        pair(lambda p: piece(T.HI, arr, p), lambda p: piece(T.ABF, arr, p), ["HI%d" % arr, "ABF%d" % arr])
 
     for t in range(ST):
         pa, pi, last = t % 2, 1 - t % 2, t == ST - 1
-        Yc = T.Y if t else T.X0
-        stages = ["GH2", "GH3", "GH0", "GH1"] if last else ["PAB0", "STG0", "STG1", "STG0"]
-        want = T.FL[:, 128:192]
+        stages = ["GH2", "GH3", "STG0", "GH0"] if last else free + free
+        Y, ys, Yn, yn = T["Y%d" % pa], yk[pa], T["Y%d" % pi], yk[pi]
+        others = ["GH0", "GH1"] if last else ["STG0", "STG1"]
+        swap = T.C[:, 512:768]
+        ahead = {0: T.STG[:, 512:640], 1: T.C[:, 0:128]}
+        akey = {0: "STG1", 1: "C0"}
+        mine, mkey = (T.ABT, ["ABT"]) if last else (T.ABF, ["ABF0", "ABF1"])
 
-        def at(arr, p):
-            return T.W[:].indirect(piece(T.OFF, arr, p))
+        def place(o, p):
+            return (lambda b, c0: b[:, c0 + p:c0 + 128:2] if last else b[:, c0 + 64 * p:c0 + 64 * p + 64])(*o)
+
+        def wrap(out, mat, src, c0, start, stop):
+            return [(out, bc(i, mat), src[:, c0 + 64 * i:c0 + 64 * (i + 1)] if last else src[:, c0 + i:c0 + G:16], start and i == 0, stop and i == 15)
+                    for i in range(16)]
+
+        def at(arr, p, a=0, b=64):
+            return T.W[:].indirect(piece(T.OFF, arr, p, a, b))
 
         def lead():
-            act(T.WA4[:], at(0, pa), ACT.Identity, bias=4.0, r=allw, w=["WA4"])
+            act(T.WA4[:], at(0, pa), ACT.Identity, bias=4.0, r=allw + ["OFF0"], w=["WA4"])
+
+        def lay_b():
+            for h in range(2):
+                spread(others[h], pi, h, True, False, 1)
+                spread("STG%d" % h, pa, h, True, False, 1)
+
+        def lay_others():
+            for h in range(2):
+                spread(others[h], pi, h, not last, True)
+                evac(others[h], h, pi)
+
+        def lay_turn():
+            for h in range(2):
+                spread("STG%d" % h, pa, h, not last, False)
 
         def gap(p):
-            tt(T.GA[:, p::2], at(0, p), Yc[:, p::2], ALU.subtract, r=allw + ys, w=["GA%d" % p])
+            tt(T.GA[:, p::2], at(0, p), Y[:, p::2], ALU.subtract, r=allw + ys + ["OFF0"], w=["GA%d" % p])
 
-        def clip():
-            ts(T.D[:], T.GA[:], 2.0, ALU.max, 7.0, ALU.min, r=["GA0", "GA1"], w=["D"])
+        def clip(p):
+            ts(T.D[:, p::2], T.GA[:, p::2], 2.0, ALU.max, 7.0, ALU.min, r=["GA%d" % p], w=["D%d" % p])
 
         def passing(p):
-            tt(T.MP[:, G * p:G * (p + 1)], at(1, p), Yc[:, p::2], ALU.is_le, r=allw + ys, w=["MP%d" % p])
+            tt(T.MP[:, G * p:G * (p + 1)], at(1, p), Y[:, p::2], ALU.is_le, r=allw + ys + ["OFF1"], w=["MP%d" % p])
 
         def own_votes(p):
-            mm(wrap(T.PCD[:, 256 + 64 * p:320 + 64 * p], T.BC, T.MP, G * p, True), ["BC", "MP%d" % p], ["PCD0"])
+            mm(wrap(T.C[:, 256 + 64 * p:320 + 64 * p], T.BC, T.MP, G * p, True, True), ["BC", "MP%d" % p], ["C0"])
 
-        def marks():
-            passing(pa)
+        def pass_votes():
             for h in range(2):
                 key = "STG%d" % h
-                lst = [(bank(key), bc(3), T.MP[:, G * pa + 512 * h:G * pa + 512 * (h + 1)], last, False)]
-                mm(lst + (spread(key, 64 * pa + 32 * h, True) if last else []), ["BC", "UN", "Z", "MP%d" % pa], [key])
-            if not last:
-                own_votes(pa)
-            tt(T.MC[:], at(1, pa), T.WA4[:], ALU.is_gt, r=allw + ["WA4"], w=["MC"])
+                mm([(bank(key), bc(3), T.MP[:, G * pa + 512 * h:G * pa + 512 * (h + 1)], False, False)], ["BC", "MP%d" % pa], [key])
+
+        def changing():
             for h in range(2):
-                key = "STG%d" % h
-                mm([(bank(key), bc(2), T.MC[:, 512 * h:512 * (h + 1)], False, True)], ["BC", "MC"], [key])
+                key, cols = "STG%d" % h, slice(512 * h, 512 * (h + 1))
+                tt(T.MC[:, cols], at(1, pa, 32 * h, 32 * h + 32), T.WA4[:, cols], ALU.is_gt, r=allw + ["WA4", "OFF1"], w=["MC%d" % h])
+                mm([(bank(key), bc(2), T.MC[:, cols], False, True)], ["BC", "MC%d" % h], [key])
                 evac(key, h, pa)
-            if last:
-                own_votes(pa)
-            mm(wrap(T.PCD[:, 384:448], T.BC, T.MC, 0, True), ["BC", "MC"], ["PCD0"])
+
+        def want_votes():
+            mm(wrap(T.C[:, 384:448], T.BC, T.MC, 0, True, True), ["BC", "MC0", "MC1"], ["C0"])
 
         def flags():
-            ts(T.FL[:], T.PCD[:, 256:448], 8.5, ALU.is_ge, w=["FL"], x=["PCD0"])
+            ts(T.FL[:], T.C[:, 256:448], 8.5, ALU.is_ge, w=["FL"], x=["C0"])
 
         def stage(k):
-            mm([(bank(stages[k]), T.IB[:], T.D[:, 512 * k:512 * (k + 1)], not last, True)], ["IB", "D"], [stages[k]])
+            mm([(bank(stages[k]), T.IB[:], T.D[:, 512 * k:512 * (k + 1)], True, True)], ["IB", "D0", "D1"], [stages[k]])
 
         def move(k):
             cols = slice(512 * k, 512 * (k + 1))
+            tt(Yn[:, cols], bank(stages[k]), Y[:, cols], ALU.add, r=[ys[k]], w=[yn[k]], x=[stages[k]])
             if last:
-                tt(T.YX[:, cols], bank(stages[k]), Yc[:, cols], ALU.add, r=[ys[k]], w=["YX%d" % k], x=[stages[k]])
-                dma("s", T.yx[:, cols], T.YX[:, cols], "dy", r=["YX%d" % k])
+                dma("s", T.yx[:, cols], Yn[:, cols], "dy", r=[yn[k]])
             else:
-                tt(T.Y[:, cols], bank(stages[k]), Yc[:, cols], ALU.add, r=[ys[k]], w=[ys[k]], x=[stages[k]])
-                dma("s", T.W[:, cols], T.Y[:, cols], "dc%d" % k, r=[ys[k]], w=[own[k]])
+                dma("s", T.W[:, cols], Yn[:, cols], "dc%d" % k, r=[yn[k]], w=[own[k]])
 
         def look(e, arr, p, a=0, b=64):
             c0 = G * (2 * p + arr)
-            o, src = T.GP[:, c0 + 16 * a:c0 + 16 * b], T.P[:].indirect(piece(T.OFF, arr, p, a, b))
-            if e == "a":
-                act(o, src, ACT.Copy, r=allp, w=gp(arr, p))
-            else:
-                cp(o, src, r=allp, w=gp(arr, p)[:1] if b < 64 else gp(arr, p))
+            keys = gp(arr, p) if (a, b) == (0, 64) else [gp(arr, p)[e == "a"]]
+            if a < b:
+                copy(e, T.GP[:, c0 + 16 * a:c0 + 16 * b], T.P[:].indirect(piece(T.OFF, arr, p, a, b)), r=allp + ["OFF%d" % arr], w=keys)
 
         def gp(arr, p):
             return ["GP%d%dv" % (arr, p), "GP%d%da" % (arr, p)]
@@ -325,122 +381,467 @@ def rank_program(g, core, T, topo):
         def gone(p):
             return T.FL[:, 64 * p:64 * p + 64]
 
-        def whole(o, arr, p):
-            return [(o, T.IB[:], piece(T.HI, arr, p), True, False), (o, T.IB[:], piece(T.LO, arr, p), False, False)]
+        def turned():
+            for arr, mat in ((0, T.WE), (1, T.WF)):
+                mm([(T.GH[:, 1024 + 128 * arr:1152 + 128 * arr], bc(i, mat), T.P[:, 128 * i:128 * (i + 1)], i == 0, i == 15) for i in range(16)],
+                   ["WM"] + allp, ["GH2"])
 
-        def cand_d(p):
-            o = piece(T.PCD, 1, p)
-            lst = [(o, si[24 * K], want, False, False), (o, si[-24 * K], gone(p), False, False)] if p == pa else []
-            mm(whole(o, 0, p) + lst + [(o, si[-K], T.ONE[:], False, True)], ["IB", "SI", "HI", "LO", "FL", "ONE"], ["PCD0"])
+        def turned_out():
+            act(T.ABT[:], T.GH[:, 1024:1280], ACT.Copy, w=["ABT"], x=["GH2"])
 
-        def cand_c(p):
-            o = piece(T.PCD, 0, p)
-            lst = [(o, si[-1296 * K], gone(p), False, False)] + ([(o, si[1152 * K], want, False, False)] if p == pa else [])
-            mm(whole(o, 1, p) + lst + wrap(o, T.WC, T.GP, G * (2 * p + 1), False), ["IB", "SI", "HI", "LO", "FL", "WC"] + gp(1, p), ["PCD0"])
+        def swap_open():
+            mm([(swap, si[-K], T.ONE[:], True, False)] + [(T.C[:, 512 + 128 * arr:640 + 128 * arr], T.IF[:], side_(mine, 1 - arr), False, False) for arr in range(2)],
+               ["IF", "SI", "ONE"] + mkey, ["C1"])
 
-        def cand_b(p):
-            o = piece(T.PAB, 1, p)
-            mm([(o, si[136 * K], gone(p), True, False)] + wrap(o, T.WA, T.GP, G * (2 * p + 1), False), ["SI", "FL", "WA"] + gp(1, p), ["PAB0"])
+        def swap_flags():
+            lst = []
+            for arr in range(2):
+                o = (T.C, 512 + 128 * arr)
+                lst += [(place(o, pa), si[24 * K], T.FL[:, 128:192], False, False)] + [(place(o, p), si[-72 * K], gone(p), False, False) for p in range(2)]
+            mm(lst, ["SI", "FL"], ["C1"])
 
-        def cand_a(p):
-            mm(wrap(piece(T.PAB, 0, p), T.WA, T.GP, G * 2 * p, True), ["WA"] + gp(0, p), ["PAB0"])
+        def swap_close():
+            mm([(T.C[:, 512:640], si[24 * K], T.CB[:], False, True)], ["SI", "CB"], ["C1"])
 
-        def ghost_open(k):
-            mm([(bank("GH%d" % k), T.IF[:], T.W[:, V + 512 * k:V + 512 * (k + 1)], True, False)], ["IF", "Wg%d" % (1 + k // 2)], ["GH%d" % k])
+        def cand_b(p, start, stop):
+            o = place((T.C, 0), p)
+            mm(wrap(o, T.WA, T.GP, G * (2 * p + 1), start, False) + [(o, si[136 * K], gone(p), False, stop)], ["SI", "FL", "WM"] + gp(1, p), ["C0"])
 
-        def ghost_add(d):
-            for k in (2 * d - 2, 2 * d - 1):
-                mm([(bank("GH%d" % k), T.IB[:], T["L%d" % (t + 1)][:, 512 * k:512 * (k + 1)], False, True)], ["IB", "L%d_%d" % (t + 1, d)], ["GH%d" % k])
+        def b_changes():
+            ts(T.CB[:], ahead[1], float(K), ALU.is_ge, w=["CB"], x=["C0"])
 
-        def ghost_out(d):
-            c0 = (d - 1) * G
-            act(T.W[:, V + c0:V + c0 + G], T.GH[:, c0:c0 + G], ACT.Copy, w=["Wg%d" % d], x=["GH%d" % (2 * d - 2), "GH%d" % (2 * d - 1)])
+        def cand_a(p, start, stop):
+            mm(wrap(place((T.STG, 512), p), T.WA, T.GP, G * 2 * p, start, stop), ["WM"] + gp(0, p), ["STG1"])
 
         def best():
-            tt(T.M[:], T.PCD[:, 0:256], T.AB[:], ALU.max, r=["AB"], w=["M"], x=["PCD0"])
+            tt(T.M[:], swap, mine[:], ALU.max, r=mkey, w=["M"], x=["C1"])
 
-        cp(T.HI[:], T.AB[:], r=["AB"], w=["HI"])
-        tt(T.LO[:], T.AB[:], T.HI[:], ALU.subtract, r=["AB", "HI"], w=["LO"])
+        def choose(arr):
+            tt(side_(T.TG, arr), ahead[arr], side_(T.M, arr), ALU.max, r=["M"], w=["TG%d" % arr], x=[akey[arr]])
+
+        def strip(arr):
+            ts(side_(T.AB, arr), side_(T.TG, arr), K - 1, ALU.bitwise_and, r=["TG%d" % arr], w=["AB%d" % arr])
+
+        def offsets(arr):
+            cp(side_(T.OFF, arr), side_(T.AB, arr), r=["AB%d" % arr], w=["OFF%d" % arr])
+
+        def floats(arr):
+            cp(side_(T.ABF, arr), side_(T.AB, arr), r=["AB%d" % arr], w=["ABF%d" % arr])
+
+        def result(arr):
+            cp(side_(T.TF, arr), side_(T.AB, arr), r=["AB%d" % arr], w=["TF%d" % arr])
+            dma("sa"[arr], (T.ya, T.yb)[arr][:], side_(T.TF, arr), "dy", r=["TF%d" % arr])
+
+        def ghost_open(ks):
+            for k in ks:
+                mm([(bank("GH%d" % k), T.IF[:], T.W[:, V + 512 * k:V + 512 * (k + 1)], True, False)], ["IF", gk[k]], ["GH%d" % k])
+
+        def ghost_add(k):
+            mm([(bank("GH%d" % k), T.IB[:], T["L%d" % (t + 1)][:, 512 * k:512 * (k + 1)], k not in OPEN, True)],
+               ["IB", "L%d_%d" % (t + 1, 1 + k // 2)], ["GH%d" % k])
+
+        def ghost_out(k):
+            o = T.W[:, V + 512 * k:V + 512 * (k + 1)]
+            if k in OPEN:
+                act(o, bank("GH%d" % k), ACT.Copy, w=[gk[k]], x=["GH%d" % k])
+            else:
+                tt(o, bank("GH%d" % k), o, ALU.add, r=[gk[k]], w=[gk[k]], x=["GH%d" % k])
+
+        def moves(e, d, a, b):
+            c0 = (d - 1) * 64
+            if a < b:
+                copy(e, T["S%d" % (t + 1)][:, 16 * (c0 + a):16 * (c0 + b)], T.D[:].indirect(T.SN[:, c0 + a:c0 + b]), r=["D0", "D1", "SN"],
+                     w=["S%d%d%s" % (t, d, e)])
+
+        def send_moves(d):
+            cols = slice((d - 1) * G, d * G)
+            send(d, T["L%d" % (t + 1)][:, cols], T["S%d" % (t + 1)][:, cols], "ar%d_%d" % (t + 1, d), ["S%d%d%s" % (t, d, e) for e in "av"])
+
         if t == 0:
-            cp(T.W[:, 0:V], T.X0[:], r=["X0"], w=own)
-            ts(T.WA[:], T.BC[:], T.WK[:, 0:1], ALU.mult, r=["BC", "WK"], w=["WA"])
-            ts(T.WC[:], T.BC[:], T.WK[:, 1:2], ALU.mult, r=["BC", "WK"], w=["WC"])
-            fill(T.BIT[:], 2.0 * ST / K, "BIT")
-        elif last:
+            high(0)
+            pieces(0)
+            zed()
+            lay_others()
+            lay_turn()
+            swap_open()
             lead()
-        else:
-            ghost_open(0)
-            ghost_open(1)
-        pair(lambda p: piece(T.HI, 0, p), lambda p: piece(T.LO, 0, p), ["HI", "LO"])
-        if t and not last:
+            ghost_open(OPEN)
+        elif not last:
+            high(0)
+            pieces(0)
             lead()
-            ghost_open(2)
-        for h in range(2):
-            key = ("GH%d" if last else "STG%d") % h
-            mm(spread(key, 64 * pi + 32 * h, False), ["UN", "Z"], [key])
-            evac(key, h, pi)
+            zed()
+            swap_open()
+            lay_others()
+            ghost_open(OPEN[:1])
+            lay_turn()
+            ghost_open(OPEN[1:])
         if not last:
-            if t:
-                ghost_open(3)
+            gap(0)
+            gap(1)
+            clip(0)
+            clip(1)
+            moves("a", 1, 0, 64)
+            moves("v", 2, 0, SENDV)
+            send_moves(1)
+            moves("a", 2, SENDV, 64)
+            send_moves(2)
+            stage(0)
+            stage(1)
+            passing(pa)
+            pass_votes()
+            changing()
+            own_votes(pa)
+            want_votes()
+            passing(pi)
+            own_votes(pi)
+            move(0)
+            look("a", 1, 0)
+            look("v", 1, 1)
+            look("a", 0, 0)
+            stage(2)
+            flags()
+            move(1)
+            move(2)
+            cand_b(0, True, False)
+            cand_b(1, False, True)
+            stage(3)
+            swap_flags()
+            b_changes()
+            move(3)
+            look("v", 0, 1, 0, SPLIT)
+            look("a", 0, 1, SPLIT, 64)
+            cand_a(0, True, False)
+            swap_close()
+            ghost_add(0)
+            ghost_add(1)
+            cand_a(1, False, True)
+            best()
+            ghost_out(0)
+            ghost_out(1)
+            choose(1)
+            choose(0)
+            strip(1)
+            strip(0)
+            floats(1)
+            if t == ST - 2:
+                high(1)
+            ghost_add(2)
+            ghost_add(3)
+            offsets(0)
+            floats(0)
+            ghost_out(2)
+            ghost_out(3)
+            offsets(1)
+            if t == ST - 2:
+                pieces(1)
+                zed(1)
+        else:
+            high(0)
+            pieces(0)
+            lay_b()
+            lead()
+            zed(0)
+            passing(pa)
+            lay_others()
+            lay_turn()
+            pass_votes()
+            changing()
+            passing(pi)
+            own_votes(pa)
+            want_votes()
+            own_votes(pi)
+            turned()
+            look("a", 1, 0)
+            look("a", 1, 1)
+            turned_out()
+            look("a", 0, 0)
+            gap(0)
+            gap(1)
+            flags()
+            clip(0)
+            clip(1)
+            cand_b(0, True, False)
+            cand_b(1, False, True)
+            stage(0)
+            stage(1)
+            swap_open()
+            stage(2)
+            stage(3)
+            swap_flags()
+            move(0)
+            b_changes()
+            cand_a(0, True, False)
+            swap_close()
+            move(1)
+            move(2)
+            move(3)
+            look("v", 0, 1, 0, SPLITL)
+            look("a", 0, 1, SPLITL, 64)
+            cand_a(1, False, True)
+            best()
+            choose(1)
+            strip(1)
+            choose(0)
+            result(1)
+            strip(0)
+            result(0)
+
+    for e in cnt:
+        wait("g", ("c" + e, cnt[e]))
+    for s in total:
+        wait("g", (s, total[s]))
+    return
+    for t in range(ST):
+        pa, pi, last = t % 2, 1 - t % 2, t == ST - 1
+        stages = ["GH2", "GH3", "GH0", "GH1"] if last else (free + ["STG0", "STG1", "STG0", "STG1"])[:4]
+        arrs = (0, 1) if last else (0,)
+        want = T.FL[:, 128:192]
+
+        def place(buf, arr, p):
+            return buf[:, 128 * arr + p:128 * (arr + 1):2] if last else piece(buf, arr, p)
+
+        def wrap(out, mat, src, c0, first_):
+            return [(out, bc(i, mat), src[:, c0 + 64 * i:c0 + 64 * (i + 1)] if last else src[:, c0 + i:c0 + G:16], first_ and i == 0, i == 15)
+                    for i in range(16)]
+
+        def at(arr, p, a=0, b=64):
+            return T.W[:].indirect(piece(T.OFF, arr, p, a, b))
+
+        def lead():
+            act(T.WA4[:], at(0, pa), ACT.Identity, bias=4.0, r=allw, w=["WA4"])
+
+        def high(arr):
+            for p in range(2):
+                act(piece(T.HI, arr, p), piece(T.ABF, arr, p), ACT.Copy, r=["ABF"], w=["HI%d" % arr])
+
+        def pieces(arr):
+            pair(lambda p: piece(T.HI, arr, p), lambda p: piece(T.ABF, arr, p), ["HI%d" % arr, "ABF"])
+
+        def lay_others():
+            for h in range(2):
+                key = ("GH%d" if last else "STG%d") % h
+                spread(key, pi, h, False, arrs)
+                evac(key, h, pi)
+
+        def lay_turn():
+            for h in range(2):
+                spread("STG%d" % h, pa, h, True, arrs)
+
+        def gap(p):
+            tt(T.GA[:, p::2], at(0, p), T.Y[:, p::2], ALU.subtract, r=allw + ys, w=["GA%d" % p])
+
+        def clip():
+            ts(T.D[:], T.GA[:], 2.0, ALU.max, 7.0, ALU.min, r=["GA0", "GA1"], w=["D"])
+
+        def passing(p):
+            tt(T.MP[:, G * p:G * (p + 1)], at(1, p), T.Y[:, p::2], ALU.is_le, r=allw + ys, w=["MP%d" % p])
+
+        def own_votes(p):
+            mm(wrap(T.CS[:, 256 + 64 * p:320 + 64 * p], T.BC, T.MP, G * p, True), ["BC", "MP%d" % p], ["CS0"])
+
+        def pass_votes():
             for h in range(2):
                 key = "STG%d" % h
-                mm([(bank(key), T.IB[:], T.ZER[:], True, False)] + spread(key, 64 * pa + 32 * h, True), ["UN", "Z", "IB", "ZER"], [key])
-            if t == 0:
-                lead()
-                for k in range(4):
-                    ghost_open(k)
+                mm([(bank(key), bc(3), T.MP[:, G * pa + 512 * h:G * pa + 512 * (h + 1)], False, False)], ["BC", "MP%d" % pa], [key])
+
+        def changing():
+            for h in range(2):
+                key, cols = "STG%d" % h, slice(512 * h, 512 * (h + 1))
+                tt(T.MC[:, cols], at(1, pa, 32 * h, 32 * h + 32), T.WA4[:, cols], ALU.is_gt, r=allw + ["WA4"], w=["MC%d" % h])
+                mm([(bank(key), bc(2), T.MC[:, cols], False, True)], ["BC", "MC%d" % h], [key])
+                evac(key, h, pa)
+
+        def want_votes():
+            mm(wrap(T.CS[:, 384:448], T.BC, T.MC, 0, True), ["BC", "MC0", "MC1"], ["CS0"])
+
+        def flags():
+            ts(T.FL[:], T.CS[:, 256:448], 8.5, ALU.is_ge, w=["FL"], x=["CS0"])
+
+        def stage(k):
+            mm([(bank(stages[k]), T.IB[:], T.D[:, 512 * k:512 * (k + 1)], True, True)], ["IB", "D"], [stages[k]])
+
+        def move(k):
+            cols = slice(512 * k, 512 * (k + 1))
+            tt(T.Y[:, cols], bank(stages[k]), T.Y[:, cols], ALU.add, r=[ys[k]], w=[ys[k]], x=[stages[k]])
+            if last:
+                dma("s", T.yx[:, cols], T.Y[:, cols], "dy", r=[ys[k]])
+            else:
+                dma("s", T.W[:, cols], T.Y[:, cols], "dc%d" % k, r=[ys[k]], w=[own[k]])
+
+        def look(e, arr, p, a=0, b=64):
+            c0 = G * (2 * p + arr)
+            keys = gp(arr, p) if (a, b) == (0, 64) else [gp(arr, p)[e == "a"]]
+            if a < b:
+                copy(e, T.GP[:, c0 + 16 * a:c0 + 16 * b], T.P[:].indirect(piece(T.OFF, arr, p, a, b)), r=allp + ["OFF"], w=keys)
+
+        def gp(arr, p):
+            return ["GP%d%dv" % (arr, p), "GP%d%da" % (arr, p)]
+
+        def gone(p):
+            return T.FL[:, 64 * p:64 * p + 64]
+
+        mine, mkey = (T.ABT, "ABT") if last else (T.ABF, "ABF")
+
+        def turned():
+            for arr, mat in ((0, T.WE), (1, T.WF)):
+                mm([(T.CL[:, 256 + 128 * arr:384 + 128 * arr], bc(i, mat), T.P[:, 128 * i:128 * (i + 1)], i == 0, i == 15) for i in range(16)],
+                   ["WM"] + allp, ["CL0"])
+
+        def turned_out():
+            act(T.ABT[:], T.CL[:, 256:512], ACT.Copy, w=["ABT"], x=["CL0"])
+
+        def cand_d(p):
+            o = place(T.CS, 1, p)
+            lst = [(o, si[24 * K], want, False, False), (o, si[-24 * K], gone(p), False, False)] if p == pa else []
+            mm([(o, T.IF[:], place(mine, 0, p), True, False)] + lst + [(o, si[-K], T.ONE[:], False, True)], ["IF", "SI", mkey, "FL", "ONE"], ["CS0"])
+
+        def cand_c(p):
+            o = place(T.CS, 0, p)
+            lst = [(o, si[-1296 * K], gone(p), False, False)] + ([(o, si[1152 * K], want, False, False)] if p == pa else [])
+            mm([(o, T.IF[:], place(mine, 1, p), True, False)] + lst + wrap(o, T.WC, T.GP, G * (2 * p + 1), False),
+               ["IF", "SI", mkey, "FL", "WM"] + gp(1, p), ["CS0"])
+
+        def cand_b(p):
+            o = place(T.CL, 1, p)
+            mm([(o, si[136 * K], gone(p), True, False)] + wrap(o, T.WA, T.GP, G * (2 * p + 1), False), ["SI", "FL", "WM"] + gp(1, p), ["CL0"])
+
+        def cand_a(p):
+            mm(wrap(place(T.CL, 0, p), T.WA, T.GP, G * 2 * p, True), ["WM"] + gp(0, p), ["CL0"])
+
+        def best():
+            tt(T.M[:], T.CS[:, 0:256], mine[:], ALU.max, r=[mkey], w=["M"], x=["CS0"])
+
+        def choose():
+            tt(T.TG[:], T.CL[:, 0:256], T.M[:], ALU.max, r=["M"], w=["TG"], x=["CL0"])
+
+        def strip():
+            ts(T.AB[:], T.TG[:], K - 1, ALU.bitwise_and, r=["TG"], w=["AB"])
+
+        def offsets():
+            cp(T.OFF[:], T.AB[:], r=["AB"], w=["OFF"])
+
+        def floats():
+            cp(T.ABF[:], T.AB[:], r=["AB"], w=["ABF"])
+
+        def ghost_open(ks):
+            for k in ks:
+                mm([(bank("GH%d" % k), T.IF[:], T.W[:, V + 512 * k:V + 512 * (k + 1)], True, False)], ["IF", gk[k]], ["GH%d" % k])
+
+        def ghost_add(k):
+            mm([(bank("GH%d" % k), T.IB[:], T["L%d" % (t + 1)][:, 512 * k:512 * (k + 1)], k not in OPEN, True)],
+               ["IB", "L%d_%d" % (t + 1, 1 + k // 2)], ["GH%d" % k])
+
+        def ghost_out(k):
+            o = T.W[:, V + 512 * k:V + 512 * (k + 1)]
+            if k in OPEN:
+                act(o, bank("GH%d" % k), ACT.Copy, w=[gk[k]], x=["GH%d" % k])
+            else:
+                tt(o, bank("GH%d" % k), o, ALU.add, r=[gk[k]], w=[gk[k]], x=["GH%d" % k])
+
+        def moves(e, d, a, b):
+            c0 = (d - 1) * 64
+            if a < b:
+                copy(e, T["S%d" % (t + 1)][:, 16 * (c0 + a):16 * (c0 + b)], T.D[:].indirect(T.SN[:, c0 + a:c0 + b]), r=["D", "SN"], w=["S%d%d%s" % (t, d, e)])
+
+        def send_moves(d):
+            cols = slice((d - 1) * G, d * G)
+            send(d, T["L%d" % (t + 1)][:, cols], T["S%d" % (t + 1)][:, cols], "ar%d_%d" % (t + 1, d), ["S%d%d%s" % (t, d, e) for e in "av"])
+
+        if t == 0:
+            high(0)
+            pieces(0)
+            zed()
+            lay_others()
+            lay_turn()
+            lead()
+            ghost_open(OPEN)
+        elif not last:
+            high(0)
+            pieces(0)
+            lead()
+            zed()
+            ghost_open(OPEN[:1])
+            lay_others()
+            ghost_open(OPEN[1:])
+            lay_turn()
+        if not last:
             gap(0)
             gap(1)
             clip()
-            for d in (1, 2):
-                cols = slice((d - 1) * G, d * G)
-                sb, key = T["S%d" % (t + 1)][:, cols], "S%d_%d" % (t + 1, d)
-                act(sb, T.D[:].indirect(T.SN[:, (d - 1) * 64:d * 64]), ACT.Copy, r=["D", "SN"], w=[key])
-                send(d, T["L%d" % (t + 1)][:, cols], sb, "ar%d_%d" % (t + 1, d), [key])
-            stage(0)
-            marks()
+            moves("a", 1, 0, 64)
+            moves("v", 2, 0, SENDV)
+            send_moves(1)
+            moves("a", 2, SENDV, 64)
+            send_moves(2)
+            for k in range(len(free)):
+                stage(k)
+            passing(pa)
+            pass_votes()
+            own_votes(pa)
+            changing()
+            want_votes()
             passing(pi)
-            stage(1)
-            stage(2)
             own_votes(pi)
+            for k in range(len(free), 4):
+                stage(k)
             look("a", 1, 0)
             look("a", 1, 1)
             move(0)
             move(1)
-            stage(3)
             flags()
             move(2)
             move(3)
-            look("v", 0, 1)
-            order("v", (), gp(0, 0), ())
-            look("a", 0, 0, SPLIT, 64)
-            del wrote[gp(0, 0)[0]]
-            look("v", 0, 0, 0, SPLIT)
+            look("v", 0, 0)
             cand_d(0)
             cand_d(1)
             cand_c(0)
             cand_b(0)
-            ghost_add(1)
+            look("v", 0, 1, 0, SPLIT)
+            look("a", 0, 1, SPLIT, 64)
             cand_c(1)
             cand_b(1)
-            best()
-            cand_a(1)
             cand_a(0)
+            ghost_add(0)
+            ghost_add(1)
+            cand_a(1)
             ghost_add(2)
+            ghost_add(3)
+            best()
+            ghost_out(0)
+            choose()
             ghost_out(1)
+            strip()
             ghost_out(2)
+            ghost_out(3)
+            floats()
+            offsets()
         else:
-            marks()
-            for arr, p in ((1, 0), (1, 1), (0, 0), (0, 1)):
+            high(0)
+            high(1)
+            pieces(0)
+            lead()
+            zed(0)
+            pieces(1)
+            zed(1)
+            passing(pa)
+            lay_turn()
+            pass_votes()
+            lay_others()
+            changing()
+            turned()
+            look("a", 1, 0)
+            turned_out()
+            for arr, p in ((1, 1), (0, 0), (0, 1)):
                 look("a", arr, p)
+            own_votes(pa)
+            want_votes()
             passing(pi)
             own_votes(pi)
             gap(0)
             flags()
             gap(1)
             clip()
-            for key in stages:
-                mm([(bank(key), si[-K], T.BIT[:], True, False)], ["SI", "BIT"], [key])
             cand_d(0)
             cand_d(1)
             cand_c(0)
@@ -449,23 +850,17 @@ def rank_program(g, core, T, topo):
                 stage(k)
             cand_c(1)
             cand_b(1)
-            for k in range(4):
-                move(k)
-            best()
             cand_a(0)
             cand_a(1)
-        tt(T.TG[:], T.PAB[:, 0:256], T.M[:], ALU.max, r=["M"], w=["TG"], x=["PAB0"])
-        if not last:
-            ts(T.AB[:], T.TG[:], K - 1, ALU.bitwise_and, r=["TG"], w=["AB"])
-            cp(T.OFF[:], T.AB[:], r=["AB"], w=["OFF"])
+            move(0)
+            move(1)
+            best()
+            move(2)
+            move(3)
+            choose()
+            strip()
 
-    for b in range(4):
-        ts(T.E0[:, b::4, :], T.TG[:, b::4], K - 1, ALU.bitwise_and, r=["TG"], w=["E0"])
-    for s in range(2):
-        ts(T.E1[:, :, 16 * s:16 * s + 16], T.E0[:], side[s], ALU.mult, r=["E0", "PF", "PF5"], w=["E1"])
-    op("v", g.vector.transpose, (T.E2[:], T.E1[:]), r=["E1"], w=["E2"])
-    for p in range(2):
-        tt(T.TF[:, p::2], T.E2[:, 8 * p:8 * p + 8, 0:16], T.E2[:, 8 * p:8 * p + 8, 16:32], ALU.add, r=["E2"], w=["TF"])
+    cp(T.TF[:], T.AB[:], r=["AB"], w=["TF"])
     dma("s", T.ya[:], T.TF[:, 0:128], "dy", r=["TF"])
     dma("a", T.yb[:], T.TF[:, 128:256], "dy", r=["TF"])
     for e in cnt:

@@ -2,15 +2,16 @@ from concourse.bass import DstId, RemoteDMATransfer
 from concourse.mybir import AluOpType as ALU, AxisListType, ActivationFunctionType as ACT
 
 N, V, G, ST, K = 8, 2048, 1024, 4, 4096
-PC = 256
+NH, PC = 2, 256
 SPLIT = 8
-SPLITL = 0
-SENDV = 0
+SPLITL = 16
+DIRECT = (2, 3)
+LASTS = ()
 OPEN = (0, 2)
 
 SCRATCH = {}
-for dt_, bufs in (("float32", dict(W=2 * V, Y0=V, Y1=V, S0=V, HB=2 * PC, WA4=G, TF=256, M=256, ABF=256, ABT=256, GF=128, PMF=256, COL=144, PF=16,
-                                   IF=128, RM=16, RM2=8, WR=64, WT=64, WK=8)),
+for dt_, bufs in (("float32", dict(W=2 * V, Y0=V, Y1=V, S0=V, HB=max(NH, 1) * PC, WA4=G, TF=256, M=256, ABF=256, ABT=256, GF=128, PMF=256, COL=144,
+                                   PF=16, IF=128, RM=16, RM2=8, WR=64, WT=64, WK=8)),
                   ("bfloat16", dict(S1=V, S2=V, S3=V, L1=V, L2=V, L3=V, GA=V, D=V, MP=V, MC=G, P=2 * V, GP=2 * V, HI=256, FL=192, CB=128, GHI=128, Z=512,
                                     IB=128, BC=144, BX=128, PM=256, PMH=256, WA=144, WE=144, WF=144, UN=8 + 8 * 128, SI=4 * 128, ONE=256)),
                   ("int32", dict(X0=V, SNI=128, TN=256, AB=256, TG=256, PI=8, GLI=128, GLJ=128)), ("uint16", dict(SN=128, OFF=256))):
@@ -19,8 +20,8 @@ for dt_, bufs in (("float32", dict(W=2 * V, Y0=V, Y1=V, S0=V, HB=2 * PC, WA4=G, 
 SCRATCH.update({"E1": ("sbuf", [128, 16, 32], "float32"), "E2": ("sbuf", [128, 16, 32], "float32")})
 for name_, n_ in (("GH", 2048), ("STG", 1024), ("C", 1024)):
     SCRATCH[name_] = ("psum", [128, n_], "float32")
-SEMAPHORES = (["cv", "ca", "cp", "cg", "dx", "dsn", "dl", "dy", "ls", "h0", "h1", "dc0", "dc1", "dc2", "dc3"]
-              + ["ar%d_%d" % (t, d) for t in range(ST) for d in (1, 2)])
+SEMAPHORES = (["cv", "ca", "cp", "cg", "dx", "dsn", "dl", "dy", "ls", "dc0", "dc1", "dc2", "dc3"] + ["h%d" % j for j in range(NH)]
+              + ["ar0_1", "ar0_2"] + ["ar%d_%d" % (t, k) for t in range(1, ST) for k in range(4)])
 
 
 def helpers(T, topo, r):
@@ -41,11 +42,11 @@ def spare(topo, src, helper, dst, d):
 def helper_program(g, core, T, topo, r, d):
     dst = T.cores[(r - d) % N]
     rid, pid, _ = topo.addr(dst)
-    for j in range(2):
+    for j in range(NH):
         g.wait_ge(T.sem["h%d" % j], len(spare(topo, T.cores[r], core, dst, d)))
         c0 = V + (d - 1) * G + j * PC
         g.remote_dma(T.W[:, c0:c0 + PC], T.HB[:, j * PC:(j + 1) * PC], T.sem["ar0_%d" % d], T.sem.ls, pid, rid, topo.mask(core, dst))
-    g.wait_ge(T.sem.ls, 2 * len(topo.engines(core, dst)))
+    g.wait_ge(T.sem.ls, NH * len(topo.engines(core, dst)))
 
 
 def rank_program(g, core, T, topo):
@@ -53,7 +54,7 @@ def rank_program(g, core, T, topo):
     if rank is None:
         for r in range(N):
             for d, h in helpers(T, topo, r).items():
-                if h == core:
+                if h == core and NH:
                     helper_program(g, core, T, topo, r, d)
         return
     q = {"v": g.vector, "a": g.scalar, "p": g.tensor, "g": g, "s": g.sync}
@@ -136,18 +137,18 @@ def rank_program(g, core, T, topo):
 
     dma("s", T.X0[:], T.x0[:], "dx", w=["X0"])
     dma("a", T.SNI[:], T.snd[:], "dsn", w=["SNI"])
-    dma("a", T.TN[:, 0:128], T.la[:], "dl")
-    dma("a", T.TN[:, 128:256], T.lb[:], "dl", w=["TN"])
+    dma("s", T.TN[:, 0:128], T.la[:], "dl", r=["X0"])
+    dma("s", T.TN[:, 128:256], T.lb[:], "dl", w=["TN"])
     gk = ["Wg%d" % k for k in range(4)]
     for d in (1, 2):
         src = (rank + d) % N
         n1 = len(topo.engines(T.cores[src], core))
-        total["ar0_%d" % d] = n1 + 2 * len(topo.engines(helpers(T, topo, src)[d], core))
+        total["ar0_%d" % d] = n1 + NH * len(topo.engines(helpers(T, topo, src)[d], core))
         for k in (2 * d - 2, 2 * d - 1):
             wrote[gk[k]] = ("ar0_%d" % d, total["ar0_%d" % d])
-        for t in range(1, ST):
-            total["ar%d_%d" % (t, d)] = n1
-            wrote["L%d_%d" % (t, d)] = ("ar%d_%d" % (t, d), n1)
+            for t in range(1, ST):
+                total["ar%d_%d" % (t, k)] = n1
+                wrote["L%d_%d" % (t, k)] = ("ar%d_%d" % (t, k), n1)
 
     op("g", g.iota, (T.PI[:, 0:1], [[0, 1]], 0, 1), w=["PI0"])
     op("g", g.iota, (T.COL[:], [[1, 144]], 0, 0), w=["COL"], allow_small_or_imprecise_dtypes=True)
@@ -164,28 +165,22 @@ def rank_program(g, core, T, topo):
         ts(T.PI[:, 1 + j:2 + j], T.PI[:, 0:1], sh, ALU.logical_shift_right, m, ALU.bitwise_and, r=["PI0"], w=["PI"])
     wait("v", wrote["WR"])
     rows = (wa, we, bias, wf)
-    for j, row in enumerate(rows[:2]):
-        for c in range(8):
-            if row[c]:
-                fill(T.WR[:, 16 * j + c:16 * j + c + 1], row[c], "WR")
-    cp(T.PF[:, 0:7], T.PI[:, 0:7], r=["PI0", "PI"], w=["PF"])
-    for j, row in enumerate(rows[2:], 2):
+    for j, row in enumerate(rows):
+        if j == 2:
+            cp(T.PF[:, 0:7], T.PI[:, 0:7], r=["PI0", "PI"], w=["PF"])
         for c in range(8):
             if row[c]:
                 fill(T.WR[:, 16 * j + c:16 * j + c + 1], row[c], "WR")
     ts(T.RM[:], T.COL[:, 0:16], T.PF[:, 1:2], ALU.is_equal, r=["COL", "PF"], w=["RM"])
     ts(T.PF[:, 8:9], T.PF[:, 4:5], T.PF[:, 2:3], ALU.add, r=["PF"], w=["PG"])
     ts(T.PF[:, 9:10], T.PF[:, 5:6], 2.0, ALU.mult, T.PF[:, 2:3], ALU.add, r=["PF"], w=["PG"])
-    ts(T.IB[:], T.COL[:, 0:128], T.PF[:, 0:1], ALU.is_equal, r=["COL", "PF"], w=["IB"])
-    ts(T.BC[:], T.COL[:], -16.0, ALU.add, T.PF[:, 2:3], ALU.is_equal, r=["COL", "PF"], w=["BC"])
+    ts(T.PF[:, 7:8], T.PF[:, 3:4], -1.0, ALU.mult, 1.0, ALU.add, r=["PF"], w=["PF7"])
+    ts(T.GLJ[:], T.GLI[:], 31, ALU.bitwise_and, r=["GLI"], w=["GLJ"])
     cp(T.SN[:], T.SNI[:], r=["SNI"], w=["SN"])
     tt(T.RM2[:], T.RM[:, 0::2], T.RM[:, 1::2], ALU.add, r=["RM"], w=["RM2"])
     ts(T.BX[:], T.COL[:, 0:128], T.PF[:, 8:9], ALU.is_equal, r=["COL", "PG"], w=["BX"])
     ts(T.PF[:, 10:11], T.PF[:, 6:7], 1000.0, ALU.mult, T.PF[:, 9:10], ALU.add, r=["PF", "PG"], w=["PH"])
-    ts(T.PF[:, 7:8], T.PF[:, 3:4], -1.0, ALU.mult, 1.0, ALU.add, r=["PF"], w=["PF7"])
-    ts(T.GLJ[:], T.GLI[:], 31, ALU.bitwise_and, r=["GLI"], w=["GLJ"])
-    for j in range(len(rows)):
-        tt(T.WT[:, 16 * j:16 * j + 16], T.WR[:, 16 * j:16 * j + 16], T.RM[:], ALU.mult, r=["WR", "RM"], w=["WT"])
+    ts(T.IB[:], T.COL[:, 0:128], T.PF[:, 0:1], ALU.is_equal, r=["COL", "PF"], w=["IB"])
 
     def bc(i, mat=T.BC):
         return mat[:, 16 - i:144 - i]
@@ -193,21 +188,22 @@ def rank_program(g, core, T, topo):
     def un(i, arr=0):
         return T.UN[:, 8 + 128 * i - 6 * arr:136 + 128 * i - 6 * arr]
 
-    for i in range(8):
-        act(un(i), T.BX[:], ACT.Identity, scale=T.RM2[:, i:i + 1], r=["BX", "RM2"], w=["UN"])
     si = {s: T.SI[:, 128 * j:128 * (j + 1)] for j, s in enumerate([136 * K, 24 * K, -72 * K, -K])}
-    for s in si:
-        act(si[s], T.IB[:], ACT.Identity, scale=float(s), r=["IB"], w=["SI"])
-    act(T.IF[:], T.IB[:], ACT.Copy, r=["IB"], w=["IF"])
 
     hs = helpers(T, topo, rank)
 
     def first(d, a, b):
         c0 = (d - 1) * G
-        ts(T.S0[:, c0 + a:c0 + b], T.X0[:].indirect(T.SN[:, (c0 + a) // 16:(c0 + b) // 16]), -2.0 * ST, ALU.add, r=["X0", "SN"], w=["S0_%d_%d" % (d, a)])
-        return "S0_%d_%d" % (d, a)
+        o, i, key = T.S0[:, c0 + a:c0 + b], T.X0[:].indirect(T.SN[:, (c0 + a) // 16:(c0 + b) // 16]), "S0_%d_%d" % (d, a)
+        if key in wrote:
+            pass
+        elif d == 1:
+            ts(o, i, -2.0 * ST, ALU.add, r=["X0", "SN"], w=[key])
+        else:
+            act(o, i, ACT.Identity, bias=-2.0 * ST, r=["X0", "SN"], w=[key])
+        return key
 
-    for j in range(2):
+    def to_helpers(j):
         order("g", [first(d, j * PC, (j + 1) * PC) for d in (1, 2)], (), ())
         trs = []
         for d in (1, 2):
@@ -218,8 +214,19 @@ def rank_program(g, core, T, topo):
                                          src=T.S0[:, c0:c0 + PC], dst=T.HB[:, j * PC:(j + 1) * PC]))
             total["ls"] += len(part)
         g.remote_dma_fused(trs, local_sem=T.sem.ls)
-        c0 = j * G
-        send(j + 1, T.W[:, V + c0 + 2 * PC:V + c0 + G], T.S0[:, c0 + 2 * PC:c0 + G], "ar0_%d" % (j + 1), [first(j + 1, 2 * PC, G)])
+
+    to_helpers(0)
+    for d in (1, 2):
+        c0 = (d - 1) * G
+        send(d, T.W[:, V + c0 + NH * PC:V + c0 + G], T.S0[:, c0 + NH * PC:c0 + G], "ar0_%d" % d, [first(d, NH * PC, G)])
+        if d == 1:
+            first(2, NH * PC, G)
+            to_helpers(1)
+    for i in range(8):
+        act(un(i), T.BX[:], ACT.Identity, scale=T.RM2[:, i:i + 1], r=["BX", "RM2"], w=["UN"])
+    for s in si:
+        act(si[s], T.IB[:], ACT.Identity, scale=float(s), r=["IB"], w=["SI"])
+    act(T.IF[:], T.IB[:], ACT.Copy, r=["IB"], w=["IF"])
 
     for s in range(2):
         cols = slice(128 * s, 128 * (s + 1))
@@ -227,92 +234,117 @@ def rank_program(g, core, T, topo):
         ts(T.PMF[:, cols], T.COL[:, 0:128], 1000.0 * s - 1.0, ALU.add, T.PF[:, 10:11], ALU.is_equal, r=["COL", "PH"], w=["PMF"])
     tt(T.GF[:], T.GLJ[:], T.GHI[:], ALU.add, r=["GLJ", "GHI"], w=["GF"])
     for j in range(len(rows)):
-        op("v", g.vector.tensor_reduce, (T.WK[:, j:j + 1], T.WT[:, 16 * j:16 * j + 16], AxisListType.X, ALU.add), r=["WT"], w=["WK"])
+        tt(T.WT[:, 16 * j:16 * j + 16], T.WR[:, 16 * j:16 * j + 16], T.RM[:], ALU.mult, r=["WR", "RM"], w=["WT"])
     tt(T.PMH[:], T.PM[:], T.PMF[:], ALU.subtract, r=["PM", "PMF"], w=["PMH"])
-    side = {0: T.PF[:, 7:8], 1: T.PF[:, 3:4]}
+    upper = {0: T.PF[:, 7:8], 1: T.PF[:, 3:4]}
     for arr in range(2):
         for p in range(2):
             for s in range(2):
-                ts(T.E1[:, 8 * arr + 4 * p:8 * arr + 4 * p + 4, 16 * s:16 * s + 16], T.TN[:, 128 * arr + p:128 * (arr + 1):2], side[s], ALU.mult,
-                   r=["TN", "PF", "PF7"], w=["E1"])
-    for j, mat in ((0, T.WA), (1, T.WE), (3, T.WF)):
-        ts(mat[:], T.BC[:], T.WK[:, j:j + 1], ALU.mult, r=["BC", "WK"], w=["WM"])
-    op("v", g.vector.transpose, (T.E2[:], T.E1[:]), r=["E1"], w=["E2"])
+                ts(T.E1[:, 8 * arr + 4 * p:8 * arr + 4 * p + 4, 16 * s:16 * s + 16], T.TN[:, 128 * arr + p:128 * (arr + 1):2], upper[s], ALU.mult,
+                   r=["TN", "PF", "PF7"], w=["E1%d" % s])
+    for j in range(len(rows)):
+        op("v", g.vector.tensor_reduce, (T.WK[:, j:j + 1], T.WT[:, 16 * j:16 * j + 16], AxisListType.X, ALU.add), r=["WT"], w=["WK"])
+    op("v", g.vector.transpose, (T.E2[:], T.E1[:]), r=["E10", "E11"], w=["E2"])
+    ts(T.BC[:], T.COL[:], -16.0, ALU.add, T.PF[:, 2:3], ALU.is_equal, r=["COL", "PF"], w=["BC"])
     own = ["W%d" % k for k in range(4)]
     yk = [["Y%d%d" % (j, k) for k in range(4)] for j in range(2)]
+    parts = ["00", "01", "10", "11"]
     for b in range(4):
-        tt(T.ABF[:, b::4], T.E2[:, b::4, 0:16], T.E2[:, b::4, 16:32], ALU.add, r=["E2"], w=["ABF0", "ABF1"])
+        tt(T.ABF[:, b::4], T.E2[:, b::4, 0:16], T.E2[:, b::4, 16:32], ALU.add, r=["E2"], w=["ABF" + u for u in parts])
     ts(T.W[:, 0:V], T.X0[:], -2.0 * ST, ALU.add, r=["X0"], w=own)
-    cp(T.OFF[:], T.ABF[:], r=["ABF0", "ABF1"], w=["OFF0", "OFF1"])
+    cp(T.OFF[:], T.ABF[:], r=["ABF" + u for u in parts], w=["OFF" + u for u in parts])
+    for j, mat in ((0, T.WA), (1, T.WE)):
+        ts(mat[:], T.BC[:], T.WK[:, j:j + 1], ALU.mult, r=["BC", "WK"], w=["WM"])
     ts(T.Y0[:], T.X0[:], -2.0 * ST, ALU.add, r=["X0"], w=yk[0])
 
     def bank(key, i=0, step=1):
         c0 = 512 * int(key[-1])
         return T[key[:-1]][:, c0 + i:c0 + 512:step]
 
-    def pair(hi, whole_, r):
+    def piece(buf, arr, p=None, a=0, b=64):
+        return buf[:, 128 * arr:128 * (arr + 1)] if p is None else buf[:, 128 * arr + 64 * p + a:128 * arr + 64 * p + b]
+
+    def both(p):
+        return (0, 1) if p is None else (p,)
+
+    def keys(name, arr, p=None):
+        return ["%s%d%d" % (name, arr, u) for u in both(p)]
+
+    def pair(hi, whole, arr, p, r):
         lst = []
-        for p in range(2):
+        for u in both(p):
             for s in range(2):
-                o = T.C[:, 256 + 128 * p + s:384 + 128 * p:2]
-                lst += [(o, T.PMH[:, 128 * s:128 * s + 128], hi(p), True, False), (o, T.PMF[:, 128 * s:128 * s + 128], whole_(p), False, True)]
+                o = T.C[:, 256 + 128 * u + s:384 + 128 * u:2]
+                lst += [(o, T.PMH[:, 128 * s:128 * s + 128], piece(hi, arr, u), True, False),
+                        (o, T.PMF[:, 128 * s:128 * s + 128], piece(whole, arr, u), False, True)]
         mm(lst, ["PMH", "PMF"] + r, ["C0"])
 
-    def zed(arr=0):
-        act(T.Z[:, 256 * arr:256 * (arr + 1)], T.C[:, 256:512], ACT.Copy, w=["Z%d" % arr], x=["C0"])
+    def high(arr, p=None):
+        act(piece(T.HI, arr, p), piece(T.ABF, arr, p), ACT.Copy, r=keys("ABF", arr, p), w=keys("HI", arr, p))
+
+    def pieces(arr, p=None):
+        pair(T.HI, T.ABF, arr, p, keys("HI", arr, p) + keys("ABF", arr, p))
+
+    def zed(arr, p=None):
+        a, b = (0, 256) if p is None else (128 * p, 128 * p + 128)
+        act(T.Z[:, 256 * arr + a:256 * arr + b], T.C[:, 256 + a:256 + b], ACT.Copy, w=keys("Z", arr, p), x=["C0"])
 
     def spread(key, p, h, start, stop, arr=0):
         c0 = 256 * arr + 128 * p + 64 * h
-        mm([(bank(key, i, 8), un(i, arr), T.Z[:, c0:c0 + 64], start and i == 0, stop and i == 7) for i in range(8)], ["UN", "Z%d" % arr], [key])
+        mm([(bank(key, i, 8), un(i), T.Z[:, c0:c0 + 64], start and i == 0, stop and i == 7) for i in range(8)], ["UN"] + keys("Z", arr, p), [key])
 
     def evac(key, h, p, ghost=0):
         act(T.P[:, V * ghost + G * h + p:V * ghost + G * (h + 1):2], bank(key), ACT.Relu, bias=T.WK[:, 2:3], r=["WK"], w=["P%d%d%d" % (ghost, p, h)], x=[key])
 
-    pair(lambda p: T.GHI[:, 64 * p:64 * p + 64], lambda p: T.GF[:, 64 * p:64 * p + 64], ["GHI", "GF"])
-    zed()
-    for p in range(2):
-        for h in range(2):
-            key = "GH%d" % (2 * p + h)
-            spread(key, p, h, True, True)
-            evac(key, h, p, 1)
+    pair(T.GHI, T.GF, 0, None, ["GHI", "GF"])
+    zed(1)
+
+    def lay_ghosts():
+        for p in range(2):
+            for h in range(2):
+                spread("GH%d" % (2 * p + h), p, h, True, True, 1)
+
+    def ghosts_out():
+        for p in range(2):
+            for h in range(2):
+                evac("GH%d" % (2 * p + h), h, p, 1)
+
     allp = ["P%d%d%d" % (a, b, c) for a in range(2) for b in range(2) for c in range(2)]
     allw = own + gk
     free = ["GH%d" % k for k in range(4) if k not in OPEN]
 
-    def piece(buf, arr, p, a=0, b=64):
-        return buf[:, 128 * arr + 64 * p + a:128 * arr + 64 * p + b]
+    def at(arr, p, a=0, b=64):
+        return T.W[:].indirect(piece(T.OFF, arr, p, a, b))
 
-    def side_(buf, arr):
-        return buf[:, 128 * arr:128 * (arr + 1)]
+    def gap(t, p, a=0, b=64):
+        tt(T.GA[:, 32 * a + p:32 * b:2], at(0, p, a, b), T["Y%d" % (t % 2)][:, 32 * a + p:32 * b:2], ALU.subtract,
+           r=allw + yk[t % 2][a // 16:b // 16] + keys("OFF", 0, p), w=["GA%d%d" % (p, a)])
 
-    def high(arr):
-        act(side_(T.HI, arr), side_(T.ABF, arr), ACT.Copy, r=["ABF%d" % arr], w=["HI%d" % arr])
+    def passing(t, p, a=0, b=64):
+        tt(T.MP[:, G * p + 16 * a:G * p + 16 * b], at(1, p, a, b), T["Y%d" % (t % 2)][:, 32 * a + p:32 * b:2], ALU.is_le,
+           r=allw + yk[t % 2][a // 16:b // 16] + keys("OFF", 1, p), w=["MP%d%d" % (p, a)])
 
-    def pieces(arr):
-        pair(lambda p: piece(T.HI, arr, p), lambda p: piece(T.ABF, arr, p), ["HI%d" % arr, "ABF%d" % arr])
+    def halves(name, p):
+        return ["%s%d%d" % (name, p, a) for a in (0, 32)]
 
     for t in range(ST):
         pa, pi, last = t % 2, 1 - t % 2, t == ST - 1
-        stages = ["GH2", "GH3", "STG0", "GH0"] if last else free + free
+        stages = ["GH2", "GH3", "GH0", "GH1"] if last else free + ["STG0", "STG1"]
         Y, ys, Yn, yn = T["Y%d" % pa], yk[pa], T["Y%d" % pi], yk[pi]
         others = ["GH0", "GH1"] if last else ["STG0", "STG1"]
-        swap = T.C[:, 512:768]
-        ahead = {0: T.STG[:, 512:640], 1: T.C[:, 0:128]}
-        akey = {0: "STG1", 1: "C0"}
-        mine, mkey = (T.ABT, ["ABT"]) if last else (T.ABF, ["ABF0", "ABF1"])
+        f = pa
+        mine, mkey = (T.ABT, ["ABT0", "ABT1"]) if last else (T.ABF, ["ABF" + u for u in parts])
 
-        def place(o, p):
-            return (lambda b, c0: b[:, c0 + p:c0 + 128:2] if last else b[:, c0 + 64 * p:c0 + 64 * p + 64])(*o)
+        def place(buf, c0, p):
+            return buf[:, c0 + p:c0 + 128:2] if last else buf[:, c0 + 64 * p:c0 + 64 * p + 64]
 
         def wrap(out, mat, src, c0, start, stop):
             return [(out, bc(i, mat), src[:, c0 + 64 * i:c0 + 64 * (i + 1)] if last else src[:, c0 + i:c0 + G:16], start and i == 0, stop and i == 15)
                     for i in range(16)]
 
-        def at(arr, p, a=0, b=64):
-            return T.W[:].indirect(piece(T.OFF, arr, p, a, b))
-
-        def lead():
-            act(T.WA4[:], at(0, pa), ACT.Identity, bias=4.0, r=allw + ["OFF0"], w=["WA4"])
+        def lead(h=None):
+            a, b = (0, 64) if h is None else (32 * h, 32 * h + 32)
+            act(T.WA4[:, 16 * a:16 * b], at(0, pa, a, b), ACT.Identity, bias=4.0, r=allw + keys("OFF", 0, pa), w=keys("WA", 4, h))
 
         def lay_b():
             for h in range(2):
@@ -328,29 +360,28 @@ def rank_program(g, core, T, topo):
             for h in range(2):
                 spread("STG%d" % h, pa, h, not last, False)
 
-        def gap(p):
-            tt(T.GA[:, p::2], at(0, p), Y[:, p::2], ALU.subtract, r=allw + ys + ["OFF0"], w=["GA%d" % p])
-
         def clip(p):
-            ts(T.D[:, p::2], T.GA[:, p::2], 2.0, ALU.max, 7.0, ALU.min, r=["GA%d" % p], w=["D%d" % p])
-
-        def passing(p):
-            tt(T.MP[:, G * p:G * (p + 1)], at(1, p), Y[:, p::2], ALU.is_le, r=allw + ys + ["OFF1"], w=["MP%d" % p])
+            ts(T.D[:, p::2], T.GA[:, p::2], 2.0, ALU.max, 7.0, ALU.min, r=halves("GA", p), w=["D%d" % p])
 
         def own_votes(p):
-            mm(wrap(T.C[:, 256 + 64 * p:320 + 64 * p], T.BC, T.MP, G * p, True, True), ["BC", "MP%d" % p], ["C0"])
+            mm(wrap(T.C[:, 256 + 64 * p:320 + 64 * p], T.BC, T.MP, G * p, True, True), ["BC"] + halves("MP", p), ["C0"])
 
         def pass_votes():
             for h in range(2):
                 key = "STG%d" % h
-                mm([(bank(key), bc(3), T.MP[:, G * pa + 512 * h:G * pa + 512 * (h + 1)], False, False)], ["BC", "MP%d" % pa], [key])
+                mm([(bank(key), bc(3), T.MP[:, G * pa + 512 * h:G * pa + 512 * (h + 1)], False, False)], ["BC"] + halves("MP", pa), [key])
 
-        def changing():
+        def lay(name, p, arr, start, stop):
             for h in range(2):
-                key, cols = "STG%d" % h, slice(512 * h, 512 * (h + 1))
-                tt(T.MC[:, cols], at(1, pa, 32 * h, 32 * h + 32), T.WA4[:, cols], ALU.is_gt, r=allw + ["WA4", "OFF1"], w=["MC%d" % h])
-                mm([(bank(key), bc(2), T.MC[:, cols], False, True)], ["BC", "MC%d" % h], [key])
-                evac(key, h, pa)
+                spread("%s%d" % (name, h), p, h, start, stop, arr)
+
+        def changing(h):
+            key, cols = "STG%d" % h, slice(512 * h, 512 * (h + 1))
+            tt(T.MC[:, cols], at(1, pa, 32 * h, 32 * h + 32), T.WA4[:, cols], ALU.is_gt, r=allw + keys("WA", 4, h) + keys("OFF", 1, pa), w=["MC%d" % h])
+            mm([(bank(key), bc(2), T.MC[:, cols], False, True)], ["BC", "MC%d" % h], [key])
+
+        def turn_out(h):
+            evac("STG%d" % h, h, pa)
 
         def want_votes():
             mm(wrap(T.C[:, 384:448], T.BC, T.MC, 0, True, True), ["BC", "MC0", "MC1"], ["C0"])
@@ -359,21 +390,35 @@ def rank_program(g, core, T, topo):
             ts(T.FL[:], T.C[:, 256:448], 8.5, ALU.is_ge, w=["FL"], x=["C0"])
 
         def stage(k):
-            mm([(bank(stages[k]), T.IB[:], T.D[:, 512 * k:512 * (k + 1)], True, True)], ["IB", "D0", "D1"], [stages[k]])
+            mm([(bank(stages[k]), T.IB[:], T.D[:, 512 * k:512 * (k + 1)], not (last and k in LASTS), True)], ["IB", "D0", "D1"], [stages[k]])
+
+        def own_open(k):
+            if k in LASTS:
+                mm([(bank(stages[k]), T.IF[:], Y[:, 512 * k:512 * (k + 1)], True, False)], ["IF", ys[k]], [stages[k]])
 
         def move(k):
             cols = slice(512 * k, 512 * (k + 1))
-            tt(Yn[:, cols], bank(stages[k]), Y[:, cols], ALU.add, r=[ys[k]], w=[yn[k]], x=[stages[k]])
+            if k in DIRECT and not last:
+                tt(T.W[:, cols], bank(stages[k]), Y[:, cols], ALU.add, r=[ys[k]], w=[own[k]], x=[stages[k]])
+                return
+            if last and k in LASTS:
+                act(Yn[:, cols], bank(stages[k]), ACT.Copy, w=[yn[k]], x=[stages[k]])
+            else:
+                tt(Yn[:, cols], bank(stages[k]), Y[:, cols], ALU.add, r=[ys[k]], w=[yn[k]], x=[stages[k]])
             if last:
                 dma("s", T.yx[:, cols], Yn[:, cols], "dy", r=[yn[k]])
             else:
                 dma("s", T.W[:, cols], Yn[:, cols], "dc%d" % k, r=[yn[k]], w=[own[k]])
 
+        def second(k):
+            if k in DIRECT:
+                act(Yn[:, 512 * k:512 * (k + 1)], T.W[:, 512 * k:512 * (k + 1)], ACT.Copy, r=[own[k]], w=[yn[k]])
+
         def look(e, arr, p, a=0, b=64):
             c0 = G * (2 * p + arr)
-            keys = gp(arr, p) if (a, b) == (0, 64) else [gp(arr, p)[e == "a"]]
+            w = gp(arr, p) if (a, b) == (0, 64) else [gp(arr, p)[e == "a"]]
             if a < b:
-                copy(e, T.GP[:, c0 + 16 * a:c0 + 16 * b], T.P[:].indirect(piece(T.OFF, arr, p, a, b)), r=allp + ["OFF%d" % arr], w=keys)
+                copy(e, T.GP[:, c0 + 16 * a:c0 + 16 * b], T.P[:].indirect(piece(T.OFF, arr, p, a, b)), r=allp + keys("OFF", arr, p), w=w)
 
         def gp(arr, p):
             return ["GP%d%dv" % (arr, p), "GP%d%da" % (arr, p)]
@@ -382,63 +427,70 @@ def rank_program(g, core, T, topo):
             return T.FL[:, 64 * p:64 * p + 64]
 
         def turned():
-            for arr, mat in ((0, T.WE), (1, T.WF)):
-                mm([(T.GH[:, 1024 + 128 * arr:1152 + 128 * arr], bc(i, mat), T.P[:, 128 * i:128 * (i + 1)], i == 0, i == 15) for i in range(16)],
-                   ["WM"] + allp, ["GH2"])
+            mm([(T.STG[:, 0:128], bc(i, T.WE), T.P[:, 128 * i:128 * (i + 1)], i == 0, i == 15) for i in range(16)], ["WM"] + allp, ["STG0"])
 
         def turned_out():
-            act(T.ABT[:], T.GH[:, 1024:1280], ACT.Copy, w=["ABT"], x=["GH2"])
+            act(T.ABT[:, 0:128], T.STG[:, 0:128], ACT.Copy, w=["ABT0"], x=["STG0"])
 
         def swap_open():
-            mm([(swap, si[-K], T.ONE[:], True, False)] + [(T.C[:, 512 + 128 * arr:640 + 128 * arr], T.IF[:], side_(mine, 1 - arr), False, False) for arr in range(2)],
-               ["IF", "SI", "ONE"] + mkey, ["C1"])
+            mm([(T.C[:, 512:768], si[-K], T.ONE[:], True, False)]
+               + [(T.C[:, 512 + 128 * arr:640 + 128 * arr], T.IF[:], piece(mine, 1 - arr), False, False) for arr in range(2)], ["IF", "SI", "ONE"] + mkey, ["C1"])
 
         def swap_flags():
             lst = []
-            for arr in range(2):
-                o = (T.C, 512 + 128 * arr)
-                lst += [(place(o, pa), si[24 * K], T.FL[:, 128:192], False, False)] + [(place(o, p), si[-72 * K], gone(p), False, False) for p in range(2)]
+            for c0 in (512, 640):
+                lst += [(place(T.C, c0, pa), si[24 * K], T.FL[:, 128:192], False, False)]
+                lst += [(place(T.C, c0, p), si[-72 * K], gone(p), False, False) for p in range(2)]
             mm(lst, ["SI", "FL"], ["C1"])
 
         def swap_close():
             mm([(T.C[:, 512:640], si[24 * K], T.CB[:], False, True)], ["SI", "CB"], ["C1"])
 
-        def cand_b(p, start, stop):
-            o = place((T.C, 0), p)
-            mm(wrap(o, T.WA, T.GP, G * (2 * p + 1), start, False) + [(o, si[136 * K], gone(p), False, stop)], ["SI", "FL", "WM"] + gp(1, p), ["C0"])
+        def cand_b(p):
+            o = place(T.C, 0, p)
+            mm(wrap(o, T.WA, T.GP, G * (2 * p + 1), p == 0, False) + [(o, si[136 * K], gone(p), False, p == 1)], ["SI", "FL", "WM"] + gp(1, p), ["C0"])
 
         def b_changes():
-            ts(T.CB[:], ahead[1], float(K), ALU.is_ge, w=["CB"], x=["C0"])
+            ts(T.CB[:], T.C[:, 0:128], float(K), ALU.is_ge, w=["CB"], x=["C0"])
 
-        def cand_a(p, start, stop):
-            mm(wrap(place((T.STG, 512), p), T.WA, T.GP, G * 2 * p, start, stop), ["WM"] + gp(0, p), ["STG1"])
+        def ahead(arr, p):
+            if arr:
+                return T.C[:, 0:128], "C0"
+            if last:
+                return T.STG[:, 512:640], "STG1"
+            return (T.STG[:, 0:64], "STG0") if p == f else (T.STG[:, 512:576], "STG1")
+
+        def cand_a(p):
+            o, key = ahead(0, p)
+            mm(wrap(place(T.STG, 512, p) if last else o, T.WA, T.GP, G * 2 * p, not (last and p), p or not last), ["WM"] + gp(0, p), [key])
 
         def best():
-            tt(T.M[:], swap, mine[:], ALU.max, r=mkey, w=["M"], x=["C1"])
+            tt(T.M[:], T.C[:, 512:768], mine[:], ALU.max, r=mkey, w=["M"], x=["C1"])
 
-        def choose(arr):
-            tt(side_(T.TG, arr), ahead[arr], side_(T.M, arr), ALU.max, r=["M"], w=["TG%d" % arr], x=[akey[arr]])
+        def choose(arr, p=None):
+            o, key = ahead(arr, p)
+            tt(piece(T.TG, arr, p), o, piece(T.M, arr, p), ALU.max, r=["M"], w=keys("TG", arr, p), x=[key])
 
-        def strip(arr):
-            ts(side_(T.AB, arr), side_(T.TG, arr), K - 1, ALU.bitwise_and, r=["TG%d" % arr], w=["AB%d" % arr])
+        def strip(arr, p=None):
+            ts(piece(T.AB, arr, p), piece(T.TG, arr, p), K - 1, ALU.bitwise_and, r=keys("TG", arr, p), w=keys("AB", arr, p))
 
-        def offsets(arr):
-            cp(side_(T.OFF, arr), side_(T.AB, arr), r=["AB%d" % arr], w=["OFF%d" % arr])
+        def offsets(arr, p=None):
+            cp(piece(T.OFF, arr, p), piece(T.AB, arr, p), r=keys("AB", arr, p), w=keys("OFF", arr, p))
 
-        def floats(arr):
-            cp(side_(T.ABF, arr), side_(T.AB, arr), r=["AB%d" % arr], w=["ABF%d" % arr])
+        def floats(arr, p=None):
+            op("g", g.affine_select, (piece(T.ABF, arr, p), piece(T.AB, arr, p), [[0, 64 * len(both(p))]], ALU.is_ge, 0.0, 0, 0),
+               r=keys("AB", arr, p), w=keys("ABF", arr, p))
 
         def result(arr):
-            cp(side_(T.TF, arr), side_(T.AB, arr), r=["AB%d" % arr], w=["TF%d" % arr])
-            dma("sa"[arr], (T.ya, T.yb)[arr][:], side_(T.TF, arr), "dy", r=["TF%d" % arr])
+            cp(piece(T.TF, arr), piece(T.AB, arr), r=keys("AB", arr), w=["TF%d" % arr])
+            dma("sa"[arr], (T.ya, T.yb)[arr][:], piece(T.TF, arr), "dy", r=["TF%d" % arr])
 
-        def ghost_open(ks):
-            for k in ks:
-                mm([(bank("GH%d" % k), T.IF[:], T.W[:, V + 512 * k:V + 512 * (k + 1)], True, False)], ["IF", gk[k]], ["GH%d" % k])
+        def ghost_open(k):
+            mm([(bank("GH%d" % k), T.IF[:], T.W[:, V + 512 * k:V + 512 * (k + 1)], True, False)], ["IF", gk[k]], ["GH%d" % k])
 
         def ghost_add(k):
             mm([(bank("GH%d" % k), T.IB[:], T["L%d" % (t + 1)][:, 512 * k:512 * (k + 1)], k not in OPEN, True)],
-               ["IB", "L%d_%d" % (t + 1, 1 + k // 2)], ["GH%d" % k])
+               ["IB", "L%d_%d" % (t + 1, k)], ["GH%d" % k])
 
         def ghost_out(k):
             o = T.W[:, V + 512 * k:V + 512 * (k + 1)]
@@ -447,107 +499,154 @@ def rank_program(g, core, T, topo):
             else:
                 tt(o, bank("GH%d" % k), o, ALU.add, r=[gk[k]], w=[gk[k]], x=["GH%d" % k])
 
-        def moves(e, d, a, b):
-            c0 = (d - 1) * 64
-            if a < b:
-                copy(e, T["S%d" % (t + 1)][:, 16 * (c0 + a):16 * (c0 + b)], T.D[:].indirect(T.SN[:, c0 + a:c0 + b]), r=["D0", "D1", "SN"],
-                     w=["S%d%d%s" % (t, d, e)])
+        def send_moves(k):
+            cols, key = slice(512 * k, 512 * (k + 1)), "S%d%d" % (t, k)
+            act(T["S%d" % (t + 1)][:, cols], T.D[:].indirect(T.SN[:, 32 * k:32 * (k + 1)]), ACT.Copy, r=["D0", "D1", "SN"], w=[key])
+            send(1 + k // 2, T["L%d" % (t + 1)][:, cols], T["S%d" % (t + 1)][:, cols], "ar%d_%d" % (t + 1, k), [key])
 
-        def send_moves(d):
-            cols = slice((d - 1) * G, d * G)
-            send(d, T["L%d" % (t + 1)][:, cols], T["S%d" % (t + 1)][:, cols], "ar%d_%d" % (t + 1, d), ["S%d%d%s" % (t, d, e) for e in "av"])
+        def turn_in(s):
+            for b in range(4):
+                ts(T.E1[:, b:8:4, 16 * s:16 * s + 16], T.ABF[:, 128 + b::4], upper[s], ALU.mult, r=keys("ABF", 1), w=["E1%d" % s])
 
+        def turn():
+            op("v", g.vector.transpose, (T.E2[:, 0:8], T.E1[:, 0:8]), r=["E10", "E11"], w=["E2"])
+
+        def turn_back():
+            for p in range(2):
+                tt(T.ABT[:, 128 + p::2], T.E2[:, 4 * p:4 * p + 4, 0:16], T.E2[:, 4 * p:4 * p + 4, 16:32], ALU.add, r=["E2"], w=["ABT1"])
+
+        if t == 0:
+            lay_ghosts();high(0);pieces(0);evac("GH0", 0, 0, 1);evac("GH1", 1, 0, 1);zed(0);evac("GH2", 0, 1, 1);evac("GH3", 1, 1, 1);lay_others();lay_turn();swap_open();lead();ghost_open(0);ghost_open(2);gap(t, pi)
+        elif not last:
+            ghost_open(0);lead();high(0, pa);lay_others();pieces(0, pa);ghost_open(2);zed(0, pa);swap_open();lay_turn()
+        if not last:
+            gap(t, pa);clip(pi);clip(pa);send_moves(1);send_moves(3);passing(t, pa);pass_votes();send_moves(0);changing(0);stage(0);send_moves(2);changing(1);turn_out(0);passing(t, pi);own_votes(pa);turn_out(1);look("a", 1, 0);want_votes();look("a", 0, f);stage(1);stage(2);move(0);own_votes(pi);ghost_add(1);look("v", 1, 1);flags();move(1);stage(3);move(2);cand_b(0);move(3);cand_b(1);look("v", 0, 1 - f, 0, SPLIT);ghost_add(3);cand_a(f);b_changes();swap_flags();swap_close();look("a", 0, 1 - f, SPLIT, 64);second(2);ghost_add(0);ghost_out(0);ghost_out(1);cand_a(1 - f);ghost_add(2);ghost_out(2);second(3);ghost_out(3);best();choose(0, f);choose(1);choose(0, 1 - f);strip(0, f);floats(0, f);strip(1);strip(0, 1 - f);offsets(0, f)
+        if t < ST - 2:
+            high(0, f);pieces(0, f);offsets(1);zed(0, f);floats(1);offsets(0, 1 - f);gap(t + 1, f, 0, 32);floats(0, 1 - f);gap(t + 1, f, 32, 64)
+        if t == ST - 2:
+            offsets(1);floats(0, 1 - f);offsets(0, 1 - f);floats(1)
+        if last:
+            high(0);passing(t, pa, 32, 64);lead(0);pieces(0);zed(0);lead(1);turn_in(1);lay("GH", pi, 0, True, True);evac("GH0", 0, pi);lay("STG", pa, 0, True, False);turn_in(0);passing(t, pa, 0, 32);pass_votes();evac("GH1", 1, pi);changing(0);turn_out(0);turn();changing(1);own_votes(pa);want_votes();turn_out(1);turned();turn_back();passing(t, pi);look("a", 1, 0);own_votes(pi);gap(t, 0);turned_out();gap(t, 1);swap_open();flags();clip(0);look("a", 1, 1);cand_b(0);cand_b(1);clip(1);look("v", 0, 1, 0, SPLITL);stage(0);move(0);stage(1);move(1);b_changes();stage(2);stage(3);move(3);move(2);look("a", 0, 0);look("a", 0, 1, SPLITL, 64);cand_a(0);swap_flags();swap_close();best();cand_a(1);choose(0);choose(1);strip(0);strip(1);result(1);result(0)
+        continue
+        if t == 0:
+            high(0);pieces(0);zed(0);lay_others();lay_turn();swap_open();lead();ghost_open(0);ghost_open(2);gap(t, pi)
+        elif not last:
+            lead();high(0, pa);ghost_open(0);ghost_open(2);lay_others();swap_open();pieces(0, pa);zed(0, pa);lay_turn()
+        if not last:
+            gap(t, pa);clip(pi);clip(pa);send_moves(0);send_moves(2);send_moves(1);send_moves(3);passing(t, pa);pass_votes();changing(0);turn_out(0);stage(0);changing(1);turn_out(1);own_votes(pa);want_votes();look("a", 1, 0);stage(1);passing(t, pi);look("a", 0, f);own_votes(pi);move(0);look("v", 1, 1);stage(2);flags();move(1);move(2);cand_b(0);cand_b(1);stage(3);look("a", 0, 1 - f, SPLIT, 64);ghost_add(0);b_changes();swap_flags();swap_close();cand_a(f);ghost_add(2);move(3);best();look("v", 0, 1 - f, 0, SPLIT);choose(0, f);choose(1);strip(0, f);ghost_out(0);ghost_out(2);ghost_add(1);floats(0, f);cand_a(1 - f);ghost_out(1);choose(0, 1 - f);offsets(0, f);high(0, f);ghost_add(3);pieces(0, f);zed(0, f);strip(1);strip(0, 1 - f);ghost_out(3)
+        if t < ST - 2:
+            offsets(1);offsets(0, 1 - f);floats(1);floats(0, 1 - f);gap(t + 1, f, 0, 32);gap(t + 1, f, 32, 64)
+        if t == ST - 2:
+            offsets(1);offsets(0, 1 - f);floats(0, 1 - f);floats(1)
+        if last:
+            high(0, pa);passing(t, pa);lead(0);turn_in(1);lead(1);lay("GH", pi, 0, True, True);pieces(0, pa);zed(0, pa);turn_in(0);lay("STG", pa, 0, True, False);pass_votes();evac("GH0", 0, pi);evac("GH1", 1, pi);changing(0);changing(1);turn_out(0);turn();gap(t, 0);own_votes(pa);want_votes();turn_out(1);passing(t, pi);turned();look("a", 1, 0);own_votes(pi);turned_out();turn_back();swap_open();gap(t, 1);flags();cand_b(0);look("a", 1, 1);clip(0);clip(1);cand_b(1);look("v", 0, 1, 0, SPLITL);stage(0);stage(2);stage(1);stage(3);b_changes();look("a", 0, 0);look("a", 0, 1, SPLITL, 64);swap_flags();move(0);swap_close();move(2);cand_a(0);move(1);best();choose(1);cand_a(1);move(3);strip(1);choose(0);result(1);strip(0);result(0)
+        continue
         if t == 0:
             high(0)
             pieces(0)
-            zed()
+            zed(0)
             lay_others()
             lay_turn()
             swap_open()
             lead()
-            ghost_open(OPEN)
+            ghost_open(OPEN[0])
+            ghost_open(OPEN[1])
+            gap(t, pi)
         elif not last:
-            high(0)
-            pieces(0)
-            lead()
-            zed()
-            swap_open()
+            high(0, pa)
             lay_others()
-            ghost_open(OPEN[:1])
+            pieces(0, pa)
+            lead()
+            zed(0, pa)
+            swap_open()
+            ghost_open(OPEN[0])
             lay_turn()
-            ghost_open(OPEN[1:])
+            ghost_open(OPEN[1])
         if not last:
-            gap(0)
-            gap(1)
-            clip(0)
-            clip(1)
-            moves("a", 1, 0, 64)
-            moves("v", 2, 0, SENDV)
+            f = pi if t == ST - 2 else pa
+            gap(t, pa)
+            clip(pi)
+            clip(pa)
             send_moves(1)
-            moves("a", 2, SENDV, 64)
             send_moves(2)
             stage(0)
             stage(1)
-            passing(pa)
+            passing(t, pa)
             pass_votes()
             changing()
             own_votes(pa)
             want_votes()
-            passing(pi)
+            passing(t, pi)
             own_votes(pi)
             move(0)
             look("a", 1, 0)
             look("v", 1, 1)
-            look("a", 0, 0)
+            look("a", 0, f)
             stage(2)
             flags()
             move(1)
             move(2)
-            cand_b(0, True, False)
-            cand_b(1, False, True)
+            cand_b(0)
+            cand_b(1)
             stage(3)
             swap_flags()
             b_changes()
             move(3)
-            look("v", 0, 1, 0, SPLIT)
-            look("a", 0, 1, SPLIT, 64)
-            cand_a(0, True, False)
+            look("v", 0, 1 - f, 0, SPLIT)
+            look("a", 0, 1 - f, SPLIT, 64)
+            cand_a(f)
             swap_close()
             ghost_add(0)
             ghost_add(1)
-            cand_a(1, False, True)
+            cand_a(1 - f)
             best()
             ghost_out(0)
             ghost_out(1)
+            choose(0, f)
             choose(1)
-            choose(0)
-            strip(1)
-            strip(0)
-            floats(1)
-            if t == ST - 2:
-                high(1)
             ghost_add(2)
             ghost_add(3)
-            offsets(0)
-            floats(0)
+            strip(0, f)
+            strip(1)
+            choose(0, 1 - f)
+            floats(0, f)
+            high(0, f)
+            pieces(0, f)
+            offsets(0, f)
             ghost_out(2)
             ghost_out(3)
-            offsets(1)
-            if t == ST - 2:
+            zed(0, f)
+            strip(0, 1 - f)
+            if t < ST - 2:
+                floats(1)
+                gap(t + 1, f, 0, 32)
+                offsets(0, 1 - f)
+                floats(0, 1 - f)
+                gap(t + 1, f, 32, 64)
+                offsets(1)
+            else:
+                floats(1)
+                offsets(1)
+                high(1)
                 pieces(1)
-                zed(1)
+                floats(0, 1 - f)
+                offsets(0, 1 - f)
+                passing(t + 1, f)
         else:
-            high(0)
-            pieces(0)
-            lay_b()
             lead()
-            zed(0)
-            passing(pa)
-            lay_others()
-            lay_turn()
+            zed(1)
+            high(0, pi)
+            lay_turn_first = [spread("STG%d" % h, pa, h, True, False) for h in range(2)]
+            pieces(0, pi)
+            zed(0, pi)
+            for h in range(2):
+                spread("STG%d" % h, pa, h, False, False, 1)
             pass_votes()
             changing()
-            passing(pi)
+            for h in range(2):
+                spread(others[h], pi, h, True, False, 1)
+            lay_others()
+            passing(t, pi)
             own_votes(pa)
             want_votes()
             own_votes(pi)
@@ -556,13 +655,13 @@ def rank_program(g, core, T, topo):
             look("a", 1, 1)
             turned_out()
             look("a", 0, 0)
-            gap(0)
-            gap(1)
+            gap(t, 0)
+            gap(t, 1)
             flags()
             clip(0)
             clip(1)
-            cand_b(0, True, False)
-            cand_b(1, False, True)
+            cand_b(0)
+            cand_b(1)
             stage(0)
             stage(1)
             swap_open()
@@ -571,14 +670,14 @@ def rank_program(g, core, T, topo):
             swap_flags()
             move(0)
             b_changes()
-            cand_a(0, True, False)
+            cand_a(0)
             swap_close()
             move(1)
             move(2)
             move(3)
             look("v", 0, 1, 0, SPLITL)
             look("a", 0, 1, SPLITL, 64)
-            cand_a(1, False, True)
+            cand_a(1)
             best()
             choose(1)
             strip(1)
@@ -587,282 +686,6 @@ def rank_program(g, core, T, topo):
             strip(0)
             result(0)
 
-    for e in cnt:
-        wait("g", ("c" + e, cnt[e]))
-    for s in total:
-        wait("g", (s, total[s]))
-    return
-    for t in range(ST):
-        pa, pi, last = t % 2, 1 - t % 2, t == ST - 1
-        stages = ["GH2", "GH3", "GH0", "GH1"] if last else (free + ["STG0", "STG1", "STG0", "STG1"])[:4]
-        arrs = (0, 1) if last else (0,)
-        want = T.FL[:, 128:192]
-
-        def place(buf, arr, p):
-            return buf[:, 128 * arr + p:128 * (arr + 1):2] if last else piece(buf, arr, p)
-
-        def wrap(out, mat, src, c0, first_):
-            return [(out, bc(i, mat), src[:, c0 + 64 * i:c0 + 64 * (i + 1)] if last else src[:, c0 + i:c0 + G:16], first_ and i == 0, i == 15)
-                    for i in range(16)]
-
-        def at(arr, p, a=0, b=64):
-            return T.W[:].indirect(piece(T.OFF, arr, p, a, b))
-
-        def lead():
-            act(T.WA4[:], at(0, pa), ACT.Identity, bias=4.0, r=allw, w=["WA4"])
-
-        def high(arr):
-            for p in range(2):
-                act(piece(T.HI, arr, p), piece(T.ABF, arr, p), ACT.Copy, r=["ABF"], w=["HI%d" % arr])
-
-        def pieces(arr):
-            pair(lambda p: piece(T.HI, arr, p), lambda p: piece(T.ABF, arr, p), ["HI%d" % arr, "ABF"])
-
-        def lay_others():
-            for h in range(2):
-                key = ("GH%d" if last else "STG%d") % h
-                spread(key, pi, h, False, arrs)
-                evac(key, h, pi)
-
-        def lay_turn():
-            for h in range(2):
-                spread("STG%d" % h, pa, h, True, arrs)
-
-        def gap(p):
-            tt(T.GA[:, p::2], at(0, p), T.Y[:, p::2], ALU.subtract, r=allw + ys, w=["GA%d" % p])
-
-        def clip():
-            ts(T.D[:], T.GA[:], 2.0, ALU.max, 7.0, ALU.min, r=["GA0", "GA1"], w=["D"])
-
-        def passing(p):
-            tt(T.MP[:, G * p:G * (p + 1)], at(1, p), T.Y[:, p::2], ALU.is_le, r=allw + ys, w=["MP%d" % p])
-
-        def own_votes(p):
-            mm(wrap(T.CS[:, 256 + 64 * p:320 + 64 * p], T.BC, T.MP, G * p, True), ["BC", "MP%d" % p], ["CS0"])
-
-        def pass_votes():
-            for h in range(2):
-                key = "STG%d" % h
-                mm([(bank(key), bc(3), T.MP[:, G * pa + 512 * h:G * pa + 512 * (h + 1)], False, False)], ["BC", "MP%d" % pa], [key])
-
-        def changing():
-            for h in range(2):
-                key, cols = "STG%d" % h, slice(512 * h, 512 * (h + 1))
-                tt(T.MC[:, cols], at(1, pa, 32 * h, 32 * h + 32), T.WA4[:, cols], ALU.is_gt, r=allw + ["WA4"], w=["MC%d" % h])
-                mm([(bank(key), bc(2), T.MC[:, cols], False, True)], ["BC", "MC%d" % h], [key])
-                evac(key, h, pa)
-
-        def want_votes():
-            mm(wrap(T.CS[:, 384:448], T.BC, T.MC, 0, True), ["BC", "MC0", "MC1"], ["CS0"])
-
-        def flags():
-            ts(T.FL[:], T.CS[:, 256:448], 8.5, ALU.is_ge, w=["FL"], x=["CS0"])
-
-        def stage(k):
-            mm([(bank(stages[k]), T.IB[:], T.D[:, 512 * k:512 * (k + 1)], True, True)], ["IB", "D"], [stages[k]])
-
-        def move(k):
-            cols = slice(512 * k, 512 * (k + 1))
-            tt(T.Y[:, cols], bank(stages[k]), T.Y[:, cols], ALU.add, r=[ys[k]], w=[ys[k]], x=[stages[k]])
-            if last:
-                dma("s", T.yx[:, cols], T.Y[:, cols], "dy", r=[ys[k]])
-            else:
-                dma("s", T.W[:, cols], T.Y[:, cols], "dc%d" % k, r=[ys[k]], w=[own[k]])
-
-        def look(e, arr, p, a=0, b=64):
-            c0 = G * (2 * p + arr)
-            keys = gp(arr, p) if (a, b) == (0, 64) else [gp(arr, p)[e == "a"]]
-            if a < b:
-                copy(e, T.GP[:, c0 + 16 * a:c0 + 16 * b], T.P[:].indirect(piece(T.OFF, arr, p, a, b)), r=allp + ["OFF"], w=keys)
-
-        def gp(arr, p):
-            return ["GP%d%dv" % (arr, p), "GP%d%da" % (arr, p)]
-
-        def gone(p):
-            return T.FL[:, 64 * p:64 * p + 64]
-
-        mine, mkey = (T.ABT, "ABT") if last else (T.ABF, "ABF")
-
-        def turned():
-            for arr, mat in ((0, T.WE), (1, T.WF)):
-                mm([(T.CL[:, 256 + 128 * arr:384 + 128 * arr], bc(i, mat), T.P[:, 128 * i:128 * (i + 1)], i == 0, i == 15) for i in range(16)],
-                   ["WM"] + allp, ["CL0"])
-
-        def turned_out():
-            act(T.ABT[:], T.CL[:, 256:512], ACT.Copy, w=["ABT"], x=["CL0"])
-
-        def cand_d(p):
-            o = place(T.CS, 1, p)
-            lst = [(o, si[24 * K], want, False, False), (o, si[-24 * K], gone(p), False, False)] if p == pa else []
-            mm([(o, T.IF[:], place(mine, 0, p), True, False)] + lst + [(o, si[-K], T.ONE[:], False, True)], ["IF", "SI", mkey, "FL", "ONE"], ["CS0"])
-
-        def cand_c(p):
-            o = place(T.CS, 0, p)
-            lst = [(o, si[-1296 * K], gone(p), False, False)] + ([(o, si[1152 * K], want, False, False)] if p == pa else [])
-            mm([(o, T.IF[:], place(mine, 1, p), True, False)] + lst + wrap(o, T.WC, T.GP, G * (2 * p + 1), False),
-               ["IF", "SI", mkey, "FL", "WM"] + gp(1, p), ["CS0"])
-
-        def cand_b(p):
-            o = place(T.CL, 1, p)
-            mm([(o, si[136 * K], gone(p), True, False)] + wrap(o, T.WA, T.GP, G * (2 * p + 1), False), ["SI", "FL", "WM"] + gp(1, p), ["CL0"])
-
-        def cand_a(p):
-            mm(wrap(place(T.CL, 0, p), T.WA, T.GP, G * 2 * p, True), ["WM"] + gp(0, p), ["CL0"])
-
-        def best():
-            tt(T.M[:], T.CS[:, 0:256], mine[:], ALU.max, r=[mkey], w=["M"], x=["CS0"])
-
-        def choose():
-            tt(T.TG[:], T.CL[:, 0:256], T.M[:], ALU.max, r=["M"], w=["TG"], x=["CL0"])
-
-        def strip():
-            ts(T.AB[:], T.TG[:], K - 1, ALU.bitwise_and, r=["TG"], w=["AB"])
-
-        def offsets():
-            cp(T.OFF[:], T.AB[:], r=["AB"], w=["OFF"])
-
-        def floats():
-            cp(T.ABF[:], T.AB[:], r=["AB"], w=["ABF"])
-
-        def ghost_open(ks):
-            for k in ks:
-                mm([(bank("GH%d" % k), T.IF[:], T.W[:, V + 512 * k:V + 512 * (k + 1)], True, False)], ["IF", gk[k]], ["GH%d" % k])
-
-        def ghost_add(k):
-            mm([(bank("GH%d" % k), T.IB[:], T["L%d" % (t + 1)][:, 512 * k:512 * (k + 1)], k not in OPEN, True)],
-               ["IB", "L%d_%d" % (t + 1, 1 + k // 2)], ["GH%d" % k])
-
-        def ghost_out(k):
-            o = T.W[:, V + 512 * k:V + 512 * (k + 1)]
-            if k in OPEN:
-                act(o, bank("GH%d" % k), ACT.Copy, w=[gk[k]], x=["GH%d" % k])
-            else:
-                tt(o, bank("GH%d" % k), o, ALU.add, r=[gk[k]], w=[gk[k]], x=["GH%d" % k])
-
-        def moves(e, d, a, b):
-            c0 = (d - 1) * 64
-            if a < b:
-                copy(e, T["S%d" % (t + 1)][:, 16 * (c0 + a):16 * (c0 + b)], T.D[:].indirect(T.SN[:, c0 + a:c0 + b]), r=["D", "SN"], w=["S%d%d%s" % (t, d, e)])
-
-        def send_moves(d):
-            cols = slice((d - 1) * G, d * G)
-            send(d, T["L%d" % (t + 1)][:, cols], T["S%d" % (t + 1)][:, cols], "ar%d_%d" % (t + 1, d), ["S%d%d%s" % (t, d, e) for e in "av"])
-
-        if t == 0:
-            high(0)
-            pieces(0)
-            zed()
-            lay_others()
-            lay_turn()
-            lead()
-            ghost_open(OPEN)
-        elif not last:
-            high(0)
-            pieces(0)
-            lead()
-            zed()
-            ghost_open(OPEN[:1])
-            lay_others()
-            ghost_open(OPEN[1:])
-            lay_turn()
-        if not last:
-            gap(0)
-            gap(1)
-            clip()
-            moves("a", 1, 0, 64)
-            moves("v", 2, 0, SENDV)
-            send_moves(1)
-            moves("a", 2, SENDV, 64)
-            send_moves(2)
-            for k in range(len(free)):
-                stage(k)
-            passing(pa)
-            pass_votes()
-            own_votes(pa)
-            changing()
-            want_votes()
-            passing(pi)
-            own_votes(pi)
-            for k in range(len(free), 4):
-                stage(k)
-            look("a", 1, 0)
-            look("a", 1, 1)
-            move(0)
-            move(1)
-            flags()
-            move(2)
-            move(3)
-            look("v", 0, 0)
-            cand_d(0)
-            cand_d(1)
-            cand_c(0)
-            cand_b(0)
-            look("v", 0, 1, 0, SPLIT)
-            look("a", 0, 1, SPLIT, 64)
-            cand_c(1)
-            cand_b(1)
-            cand_a(0)
-            ghost_add(0)
-            ghost_add(1)
-            cand_a(1)
-            ghost_add(2)
-            ghost_add(3)
-            best()
-            ghost_out(0)
-            choose()
-            ghost_out(1)
-            strip()
-            ghost_out(2)
-            ghost_out(3)
-            floats()
-            offsets()
-        else:
-            high(0)
-            high(1)
-            pieces(0)
-            lead()
-            zed(0)
-            pieces(1)
-            zed(1)
-            passing(pa)
-            lay_turn()
-            pass_votes()
-            lay_others()
-            changing()
-            turned()
-            look("a", 1, 0)
-            turned_out()
-            for arr, p in ((1, 1), (0, 0), (0, 1)):
-                look("a", arr, p)
-            own_votes(pa)
-            want_votes()
-            passing(pi)
-            own_votes(pi)
-            gap(0)
-            flags()
-            gap(1)
-            clip()
-            cand_d(0)
-            cand_d(1)
-            cand_c(0)
-            cand_b(0)
-            for k in range(4):
-                stage(k)
-            cand_c(1)
-            cand_b(1)
-            cand_a(0)
-            cand_a(1)
-            move(0)
-            move(1)
-            best()
-            move(2)
-            move(3)
-            choose()
-            strip()
-
-    cp(T.TF[:], T.AB[:], r=["AB"], w=["TF"])
-    dma("s", T.ya[:], T.TF[:, 0:128], "dy", r=["TF"])
-    dma("a", T.yb[:], T.TF[:, 128:256], "dy", r=["TF"])
     for e in cnt:
         wait("g", ("c" + e, cnt[e]))
     for s in total:

from concourse.bass import DstId, RemoteDMATransfer
from concourse.mybir import AluOpType as ALU, AxisListType, ActivationFunctionType as ACT

N, V, G, ST, K = 8, 2048, 1024, 4, 4096
NH, PC = 2, 256
SPLIT = 8
SPLITL = 16
DIRECT = (2, 3)
LASTS = ()
OPEN = (0, 2)

SCRATCH = {}
for dt_, bufs in (("float32", dict(W=2 * V, Y0=V, Y1=V, S0=V, HB=max(NH, 1) * PC, WA4=G, TF=256, M=256, ABF=256, ABT=256, GF=128, PMF=256, COL=144,
                                   PF=16, IF=128, RM=16, RM2=8, WR=64, WT=64, WK=8)),
                  ("bfloat16", dict(S1=V, S2=V, S3=V, L1=V, L2=V, L3=V, GA=V, D=V, MP=V, MC=G, P=2 * V, GP=2 * V, HI=256, FL=192, CB=128, GHI=128, Z=512,
                                    IB=128, BC=144, BX=128, PM=256, PMH=256, WA=144, WE=144, WF=144, UN=8 + 8 * 128, SI=4 * 128, ONE=256)),
                  ("int32", dict(X0=V, SNI=128, TN=256, AB=256, TG=256, PI=8, GLI=128, GLJ=128)), ("uint16", dict(SN=128, OFF=256))):
    for name_, n_ in bufs.items():
        SCRATCH[name_] = ("sbuf", [128, n_], dt_)
SCRATCH.update({"E1": ("sbuf", [128, 16, 32], "float32"), "E2": ("sbuf", [128, 16, 32], "float32")})
for name_, n_ in (("GH", 2048), ("STG", 1024), ("C", 1024)):
    SCRATCH[name_] = ("psum", [128, n_], "float32")
SEMAPHORES = (["cv", "ca", "cp", "cg", "dx", "dsn", "dl", "dy", "ls", "dc0", "dc1", "dc2", "dc3"] + ["h%d" % j for j in range(NH)]
              + ["ar0_1", "ar0_2"] + ["ar%d_%d" % (t, k) for t in range(1, ST) for k in range(4)])


def helpers(T, topo, r):
    c = T.cores[r]
    out = {}
    for d in (1, 2):
        dst = T.cores[(r - d) % N]
        out[d] = [h for h in topo.cores_of(c) if topo.die(h) != topo.die(c) and topo.may_write(h, dst)
                  and T.rank_of(h) is None and h not in out.values()][0]
    return out


def spare(topo, src, helper, dst, d):
    e = [x for x in topo.engines(src, helper) if x not in topo.engines(src, dst)]
    return e[(d - 1) * len(e) // 2:d * len(e) // 2]


def helper_program(g, core, T, topo, r, d):
    dst = T.cores[(r - d) % N]
    rid, pid, _ = topo.addr(dst)
    for j in range(NH):
        g.wait_ge(T.sem["h%d" % j], len(spare(topo, T.cores[r], core, dst, d)))
        c0 = V + (d - 1) * G + j * PC
        g.remote_dma(T.W[:, c0:c0 + PC], T.HB[:, j * PC:(j + 1) * PC], T.sem["ar0_%d" % d], T.sem.ls, pid, rid, topo.mask(core, dst))
    g.wait_ge(T.sem.ls, NH * len(topo.engines(core, dst)))


def rank_program(g, core, T, topo):
    rank = T.rank_of(core)
    if rank is None:
        for r in range(N):
            for d, h in helpers(T, topo, r).items():
                if h == core and NH:
                    helper_program(g, core, T, topo, r, d)
        return
    q = {"v": g.vector, "a": g.scalar, "p": g.tensor, "g": g, "s": g.sync}
    cnt = {"v": 0, "a": 0, "p": 0, "g": 0}
    seen = {e: {} for e in q}
    wrote, read, total = {}, {}, {"ls": 0}

    def wait(e, tok):
        if seen[e].get(tok[0], 0) < tok[1]:
            q[e].wait_ge(T.sem[tok[0]], tok[1])
            seen[e][tok[0]] = tok[1]

    def order(e, r, w, x, late=False):
        own = "c" + e
        need = {}
        toks = [wrote[k] for k in r if k in wrote and not (e == "p" and wrote[k][0] == own)]
        for k in list(w) + list(x):
            toks += read.get(k, []) + ([wrote[k]] if k in wrote and (late or wrote[k][0] != own) else [])
        for s, v in toks:
            need[s] = max(need.get(s, 0), v)
        for s in need:
            wait(e, (s, need[s]))

    def note(tok, r, w, x):
        for k in list(w) + list(x):
            wrote[k] = tok
            read[k] = []
        for k in r:
            if k not in w:
                read.setdefault(k, []).append(tok)

    def op(e, fn, args, r=(), w=(), x=(), **kw):
        order(e, r, w, x)
        cnt[e] += 1
        fn(*args, **kw).then_inc(T.sem["c" + e], 1)
        note(("c" + e, cnt[e]), r, w, x)

    def mm(lst, r, x):
        order("p", r, (), x)
        for a in lst[:-1]:
            g.tensor.matmul(*a)
        cnt["p"] += 1
        g.tensor.matmul(*lst[-1]).then_inc(T.sem.cp, 1)
        note(("cp", cnt["p"]), r, (), x)

    def dma(e, out, in_, sem, r=(), w=()):
        order(e, r, w, (), True)
        q[e].dma_start(out, in_).then_inc(T.sem[sem], 16)
        total[sem] = total.get(sem, 0) + 16
        note((sem, total[sem]), r, w, ())

    def ts(o, i, s1, o0, s2=None, o1=None, **k):
        op("v", g.vector.tensor_scalar, (o, i, s1, None, o0) if o1 is None else (o, i, s1, s2, o0, o1), **k)

    def tt(o, a, b, alu, **k):
        op("v", g.vector.tensor_tensor, (o, a, b, alu), **k)

    def cp(o, i, **k):
        op("v", g.vector.tensor_copy, (o, i), **k)

    def fill(o, c, key):
        op("v", g.vector.memset, (o, float(c)), w=[key])

    def act(o, i, f, **k):
        op("a", g.scalar.activation, (o, i, f), **k)

    def copy(e, o, i, **k):
        if e == "a":
            act(o, i, ACT.Copy, **k)
        else:
            cp(o, i, **k)

    dsts = {d: T.cores[(rank - d) % N] for d in (1, 2)}

    def send(d, out, in_, sem, r):
        order("g", r, (), ())
        rid, pid, _ = topo.addr(dsts[d])
        g.remote_dma(out, in_, T.sem[sem], T.sem.ls, pid, rid, topo.mask(core, dsts[d]))
        total["ls"] += len(topo.engines(core, dsts[d]))

    dma("s", T.X0[:], T.x0[:], "dx", w=["X0"])
    dma("a", T.SNI[:], T.snd[:], "dsn", w=["SNI"])
    dma("s", T.TN[:, 0:128], T.la[:], "dl", r=["X0"])
    dma("s", T.TN[:, 128:256], T.lb[:], "dl", w=["TN"])
    gk = ["Wg%d" % k for k in range(4)]
    for d in (1, 2):
        src = (rank + d) % N
        n1 = len(topo.engines(T.cores[src], core))
        total["ar0_%d" % d] = n1 + NH * len(topo.engines(helpers(T, topo, src)[d], core))
        for k in (2 * d - 2, 2 * d - 1):
            wrote[gk[k]] = ("ar0_%d" % d, total["ar0_%d" % d])
            for t in range(1, ST):
                total["ar%d_%d" % (t, k)] = n1
                wrote["L%d_%d" % (t, k)] = ("ar%d_%d" % (t, k), n1)

    op("g", g.iota, (T.PI[:, 0:1], [[0, 1]], 0, 1), w=["PI0"])
    op("g", g.iota, (T.COL[:], [[1, 144]], 0, 0), w=["COL"], allow_small_or_imprecise_dtypes=True)
    op("g", g.iota, (T.GHI[:], [[0, 2], [32, 64]], V, 0), w=["GHI"], allow_small_or_imprecise_dtypes=True)
    op("g", g.iota, (T.GLI[:], [[1, 2], [0, 64]], 0, 2), w=["GLI"])
    wa = [1, 1, 2 * K, -16 * K, -8, -K, 0, 0]
    bias = [0, 8, -8, -8, 1, 1, 0, 8]
    we = [1, 1, 0, 0, -8, 0, 0, 0]
    wf = [0, 0, 0, 0, -8, 0, 1, 1]
    fill(T.WR[:], 0, "WR")
    fill(T.ONE[:], 1, "ONE")
    fill(T.UN[:, 0:8], 0, "UN")
    for j, (sh, m) in enumerate(((0, 15), (0, 112), (4, 1), (0, 1), (0, 7), (3, 1))):
        ts(T.PI[:, 1 + j:2 + j], T.PI[:, 0:1], sh, ALU.logical_shift_right, m, ALU.bitwise_and, r=["PI0"], w=["PI"])
    wait("v", wrote["WR"])
    rows = (wa, we, bias, wf)
    for j, row in enumerate(rows):
        if j == 2:
            cp(T.PF[:, 0:7], T.PI[:, 0:7], r=["PI0", "PI"], w=["PF"])
        for c in range(8):
            if row[c]:
                fill(T.WR[:, 16 * j + c:16 * j + c + 1], row[c], "WR")
    ts(T.RM[:], T.COL[:, 0:16], T.PF[:, 1:2], ALU.is_equal, r=["COL", "PF"], w=["RM"])
    ts(T.PF[:, 8:9], T.PF[:, 4:5], T.PF[:, 2:3], ALU.add, r=["PF"], w=["PG"])
    ts(T.PF[:, 9:10], T.PF[:, 5:6], 2.0, ALU.mult, T.PF[:, 2:3], ALU.add, r=["PF"], w=["PG"])
    ts(T.PF[:, 7:8], T.PF[:, 3:4], -1.0, ALU.mult, 1.0, ALU.add, r=["PF"], w=["PF7"])
    ts(T.GLJ[:], T.GLI[:], 31, ALU.bitwise_and, r=["GLI"], w=["GLJ"])
    cp(T.SN[:], T.SNI[:], r=["SNI"], w=["SN"])
    tt(T.RM2[:], T.RM[:, 0::2], T.RM[:, 1::2], ALU.add, r=["RM"], w=["RM2"])
    ts(T.BX[:], T.COL[:, 0:128], T.PF[:, 8:9], ALU.is_equal, r=["COL", "PG"], w=["BX"])
    ts(T.PF[:, 10:11], T.PF[:, 6:7], 1000.0, ALU.mult, T.PF[:, 9:10], ALU.add, r=["PF", "PG"], w=["PH"])
    ts(T.IB[:], T.COL[:, 0:128], T.PF[:, 0:1], ALU.is_equal, r=["COL", "PF"], w=["IB"])

    def bc(i, mat=T.BC):
        return mat[:, 16 - i:144 - i]

    def un(i, arr=0):
        return T.UN[:, 8 + 128 * i - 6 * arr:136 + 128 * i - 6 * arr]

    si = {s: T.SI[:, 128 * j:128 * (j + 1)] for j, s in enumerate([136 * K, 24 * K, -72 * K, -K])}

    hs = helpers(T, topo, rank)

    def first(d, a, b):
        c0 = (d - 1) * G
        o, i, key = T.S0[:, c0 + a:c0 + b], T.X0[:].indirect(T.SN[:, (c0 + a) // 16:(c0 + b) // 16]), "S0_%d_%d" % (d, a)
        if key in wrote:
            pass
        elif d == 1:
            ts(o, i, -2.0 * ST, ALU.add, r=["X0", "SN"], w=[key])
        else:
            act(o, i, ACT.Identity, bias=-2.0 * ST, r=["X0", "SN"], w=[key])
        return key

    def to_helpers(j):
        order("g", [first(d, j * PC, (j + 1) * PC) for d in (1, 2)], (), ())
        trs = []
        for d in (1, 2):
            part = spare(topo, core, hs[d], dsts[d], d)
            rid, pid, _ = topo.addr(hs[d])
            c0 = (d - 1) * G + j * PC
            trs.append(RemoteDMATransfer(dst_ids=[DstId(rid=rid, pnc=pid)], dma_engine_mask=sum(1 << e for e in part), remote_sem=T.sem["h%d" % j],
                                         src=T.S0[:, c0:c0 + PC], dst=T.HB[:, j * PC:(j + 1) * PC]))
            total["ls"] += len(part)
        g.remote_dma_fused(trs, local_sem=T.sem.ls)

    to_helpers(0)
    for d in (1, 2):
        c0 = (d - 1) * G
        send(d, T.W[:, V + c0 + NH * PC:V + c0 + G], T.S0[:, c0 + NH * PC:c0 + G], "ar0_%d" % d, [first(d, NH * PC, G)])
        if d == 1:
            first(2, NH * PC, G)
            to_helpers(1)
    for i in range(8):
        act(un(i), T.BX[:], ACT.Identity, scale=T.RM2[:, i:i + 1], r=["BX", "RM2"], w=["UN"])
    for s in si:
        act(si[s], T.IB[:], ACT.Identity, scale=float(s), r=["IB"], w=["SI"])
    act(T.IF[:], T.IB[:], ACT.Copy, r=["IB"], w=["IF"])

    for s in range(2):
        cols = slice(128 * s, 128 * (s + 1))
        ts(T.PM[:, cols], T.COL[:, 0:128], 1000.0 * s, ALU.add, T.PF[:, 10:11], ALU.is_equal, r=["COL", "PH"], w=["PM"])
        ts(T.PMF[:, cols], T.COL[:, 0:128], 1000.0 * s - 1.0, ALU.add, T.PF[:, 10:11], ALU.is_equal, r=["COL", "PH"], w=["PMF"])
    tt(T.GF[:], T.GLJ[:], T.GHI[:], ALU.add, r=["GLJ", "GHI"], w=["GF"])
    for j in range(len(rows)):
        tt(T.WT[:, 16 * j:16 * j + 16], T.WR[:, 16 * j:16 * j + 16], T.RM[:], ALU.mult, r=["WR", "RM"], w=["WT"])
    tt(T.PMH[:], T.PM[:], T.PMF[:], ALU.subtract, r=["PM", "PMF"], w=["PMH"])
    upper = {0: T.PF[:, 7:8], 1: T.PF[:, 3:4]}
    for arr in range(2):
        for p in range(2):
            for s in range(2):
                ts(T.E1[:, 8 * arr + 4 * p:8 * arr + 4 * p + 4, 16 * s:16 * s + 16], T.TN[:, 128 * arr + p:128 * (arr + 1):2], upper[s], ALU.mult,
                   r=["TN", "PF", "PF7"], w=["E1%d" % s])
    for j in range(len(rows)):
        op("v", g.vector.tensor_reduce, (T.WK[:, j:j + 1], T.WT[:, 16 * j:16 * j + 16], AxisListType.X, ALU.add), r=["WT"], w=["WK"])
    op("v", g.vector.transpose, (T.E2[:], T.E1[:]), r=["E10", "E11"], w=["E2"])
    ts(T.BC[:], T.COL[:], -16.0, ALU.add, T.PF[:, 2:3], ALU.is_equal, r=["COL", "PF"], w=["BC"])
    own = ["W%d" % k for k in range(4)]
    yk = [["Y%d%d" % (j, k) for k in range(4)] for j in range(2)]
    parts = ["00", "01", "10", "11"]
    for b in range(4):
        tt(T.ABF[:, b::4], T.E2[:, b::4, 0:16], T.E2[:, b::4, 16:32], ALU.add, r=["E2"], w=["ABF" + u for u in parts])
    ts(T.W[:, 0:V], T.X0[:], -2.0 * ST, ALU.add, r=["X0"], w=own)
    cp(T.OFF[:], T.ABF[:], r=["ABF" + u for u in parts], w=["OFF" + u for u in parts])
    for j, mat in ((0, T.WA), (1, T.WE)):
        ts(mat[:], T.BC[:], T.WK[:, j:j + 1], ALU.mult, r=["BC", "WK"], w=["WM"])
    ts(T.Y0[:], T.X0[:], -2.0 * ST, ALU.add, r=["X0"], w=yk[0])

    def bank(key, i=0, step=1):
        c0 = 512 * int(key[-1])
        return T[key[:-1]][:, c0 + i:c0 + 512:step]

    def piece(buf, arr, p=None, a=0, b=64):
        return buf[:, 128 * arr:128 * (arr + 1)] if p is None else buf[:, 128 * arr + 64 * p + a:128 * arr + 64 * p + b]

    def both(p):
        return (0, 1) if p is None else (p,)

    def keys(name, arr, p=None):
        return ["%s%d%d" % (name, arr, u) for u in both(p)]

    def pair(hi, whole, arr, p, r):
        lst = []
        for u in both(p):
            for s in range(2):
                o = T.C[:, 256 + 128 * u + s:384 + 128 * u:2]
                lst += [(o, T.PMH[:, 128 * s:128 * s + 128], piece(hi, arr, u), True, False),
                        (o, T.PMF[:, 128 * s:128 * s + 128], piece(whole, arr, u), False, True)]
        mm(lst, ["PMH", "PMF"] + r, ["C0"])

    def high(arr, p=None):
        act(piece(T.HI, arr, p), piece(T.ABF, arr, p), ACT.Copy, r=keys("ABF", arr, p), w=keys("HI", arr, p))

    def pieces(arr, p=None):
        pair(T.HI, T.ABF, arr, p, keys("HI", arr, p) + keys("ABF", arr, p))

    def zed(arr, p=None):
        a, b = (0, 256) if p is None else (128 * p, 128 * p + 128)
        act(T.Z[:, 256 * arr + a:256 * arr + b], T.C[:, 256 + a:256 + b], ACT.Copy, w=keys("Z", arr, p), x=["C0"])

    def spread(key, p, h, start, stop, arr=0):
        c0 = 256 * arr + 128 * p + 64 * h
        mm([(bank(key, i, 8), un(i), T.Z[:, c0:c0 + 64], start and i == 0, stop and i == 7) for i in range(8)], ["UN"] + keys("Z", arr, p), [key])

    def evac(key, h, p, ghost=0):
        act(T.P[:, V * ghost + G * h + p:V * ghost + G * (h + 1):2], bank(key), ACT.Relu, bias=T.WK[:, 2:3], r=["WK"], w=["P%d%d%d" % (ghost, p, h)], x=[key])

    pair(T.GHI, T.GF, 0, None, ["GHI", "GF"])
    zed(1)

    def lay_ghosts():
        for p in range(2):
            for h in range(2):
                spread("GH%d" % (2 * p + h), p, h, True, True, 1)

    def ghosts_out():
        for p in range(2):
            for h in range(2):
                evac("GH%d" % (2 * p + h), h, p, 1)

    allp = ["P%d%d%d" % (a, b, c) for a in range(2) for b in range(2) for c in range(2)]
    allw = own + gk
    free = ["GH%d" % k for k in range(4) if k not in OPEN]

    def at(arr, p, a=0, b=64):
        return T.W[:].indirect(piece(T.OFF, arr, p, a, b))

    def gap(t, p, a=0, b=64):
        tt(T.GA[:, 32 * a + p:32 * b:2], at(0, p, a, b), T["Y%d" % (t % 2)][:, 32 * a + p:32 * b:2], ALU.subtract,
           r=allw + yk[t % 2][a // 16:b // 16] + keys("OFF", 0, p), w=["GA%d%d" % (p, a)])

    def passing(t, p, a=0, b=64):
        tt(T.MP[:, G * p + 16 * a:G * p + 16 * b], at(1, p, a, b), T["Y%d" % (t % 2)][:, 32 * a + p:32 * b:2], ALU.is_le,
           r=allw + yk[t % 2][a // 16:b // 16] + keys("OFF", 1, p), w=["MP%d%d" % (p, a)])

    def halves(name, p):
        return ["%s%d%d" % (name, p, a) for a in (0, 32)]

    for t in range(ST):
        pa, pi, last = t % 2, 1 - t % 2, t == ST - 1
        stages = ["GH2", "GH3", "GH0", "GH1"] if last else free + ["STG0", "STG1"]
        Y, ys, Yn, yn = T["Y%d" % pa], yk[pa], T["Y%d" % pi], yk[pi]
        others = ["GH0", "GH1"] if last else ["STG0", "STG1"]
        f = pa
        mine, mkey = (T.ABT, ["ABT0", "ABT1"]) if last else (T.ABF, ["ABF" + u for u in parts])

        def place(buf, c0, p):
            return buf[:, c0 + p:c0 + 128:2] if last else buf[:, c0 + 64 * p:c0 + 64 * p + 64]

        def wrap(out, mat, src, c0, start, stop):
            return [(out, bc(i, mat), src[:, c0 + 64 * i:c0 + 64 * (i + 1)] if last else src[:, c0 + i:c0 + G:16], start and i == 0, stop and i == 15)
                    for i in range(16)]

        def lead(h=None):
            a, b = (0, 64) if h is None else (32 * h, 32 * h + 32)
            act(T.WA4[:, 16 * a:16 * b], at(0, pa, a, b), ACT.Identity, bias=4.0, r=allw + keys("OFF", 0, pa), w=keys("WA", 4, h))

        def lay_b():
            for h in range(2):
                spread(others[h], pi, h, True, False, 1)
                spread("STG%d" % h, pa, h, True, False, 1)

        def lay_others():
            for h in range(2):
                spread(others[h], pi, h, not last, True)
                evac(others[h], h, pi)

        def lay_turn():
            for h in range(2):
                spread("STG%d" % h, pa, h, not last, False)

        def clip(p):
            ts(T.D[:, p::2], T.GA[:, p::2], 2.0, ALU.max, 7.0, ALU.min, r=halves("GA", p), w=["D%d" % p])

        def own_votes(p):
            mm(wrap(T.C[:, 256 + 64 * p:320 + 64 * p], T.BC, T.MP, G * p, True, True), ["BC"] + halves("MP", p), ["C0"])

        def pass_votes():
            for h in range(2):
                key = "STG%d" % h
                mm([(bank(key), bc(3), T.MP[:, G * pa + 512 * h:G * pa + 512 * (h + 1)], False, False)], ["BC"] + halves("MP", pa), [key])

        def lay(name, p, arr, start, stop):
            for h in range(2):
                spread("%s%d" % (name, h), p, h, start, stop, arr)

        def changing(h):
            key, cols = "STG%d" % h, slice(512 * h, 512 * (h + 1))
            tt(T.MC[:, cols], at(1, pa, 32 * h, 32 * h + 32), T.WA4[:, cols], ALU.is_gt, r=allw + keys("WA", 4, h) + keys("OFF", 1, pa), w=["MC%d" % h])
            mm([(bank(key), bc(2), T.MC[:, cols], False, True)], ["BC", "MC%d" % h], [key])

        def turn_out(h):
            evac("STG%d" % h, h, pa)

        def want_votes():
            mm(wrap(T.C[:, 384:448], T.BC, T.MC, 0, True, True), ["BC", "MC0", "MC1"], ["C0"])

        def flags():
            ts(T.FL[:], T.C[:, 256:448], 8.5, ALU.is_ge, w=["FL"], x=["C0"])

        def stage(k):
            mm([(bank(stages[k]), T.IB[:], T.D[:, 512 * k:512 * (k + 1)], not (last and k in LASTS), True)], ["IB", "D0", "D1"], [stages[k]])

        def own_open(k):
            if k in LASTS:
                mm([(bank(stages[k]), T.IF[:], Y[:, 512 * k:512 * (k + 1)], True, False)], ["IF", ys[k]], [stages[k]])

        def move(k):
            cols = slice(512 * k, 512 * (k + 1))
            if k in DIRECT and not last:
                tt(T.W[:, cols], bank(stages[k]), Y[:, cols], ALU.add, r=[ys[k]], w=[own[k]], x=[stages[k]])
                return
            if last and k in LASTS:
                act(Yn[:, cols], bank(stages[k]), ACT.Copy, w=[yn[k]], x=[stages[k]])
            else:
                tt(Yn[:, cols], bank(stages[k]), Y[:, cols], ALU.add, r=[ys[k]], w=[yn[k]], x=[stages[k]])
            if last:
                dma("s", T.yx[:, cols], Yn[:, cols], "dy", r=[yn[k]])
            else:
                dma("s", T.W[:, cols], Yn[:, cols], "dc%d" % k, r=[yn[k]], w=[own[k]])

        def second(k):
            if k in DIRECT:
                act(Yn[:, 512 * k:512 * (k + 1)], T.W[:, 512 * k:512 * (k + 1)], ACT.Copy, r=[own[k]], w=[yn[k]])

        def look(e, arr, p, a=0, b=64):
            c0 = G * (2 * p + arr)
            w = gp(arr, p) if (a, b) == (0, 64) else [gp(arr, p)[e == "a"]]
            if a < b:
                copy(e, T.GP[:, c0 + 16 * a:c0 + 16 * b], T.P[:].indirect(piece(T.OFF, arr, p, a, b)), r=allp + keys("OFF", arr, p), w=w)

        def gp(arr, p):
            return ["GP%d%dv" % (arr, p), "GP%d%da" % (arr, p)]

        def gone(p):
            return T.FL[:, 64 * p:64 * p + 64]

        def turned():
            mm([(T.STG[:, 0:128], bc(i, T.WE), T.P[:, 128 * i:128 * (i + 1)], i == 0, i == 15) for i in range(16)], ["WM"] + allp, ["STG0"])

        def turned_out():
            act(T.ABT[:, 0:128], T.STG[:, 0:128], ACT.Copy, w=["ABT0"], x=["STG0"])

        def swap_open():
            mm([(T.C[:, 512:768], si[-K], T.ONE[:], True, False)]
               + [(T.C[:, 512 + 128 * arr:640 + 128 * arr], T.IF[:], piece(mine, 1 - arr), False, False) for arr in range(2)], ["IF", "SI", "ONE"] + mkey, ["C1"])

        def swap_flags():
            lst = []
            for c0 in (512, 640):
                lst += [(place(T.C, c0, pa), si[24 * K], T.FL[:, 128:192], False, False)]
                lst += [(place(T.C, c0, p), si[-72 * K], gone(p), False, False) for p in range(2)]
            mm(lst, ["SI", "FL"], ["C1"])

        def swap_close():
            mm([(T.C[:, 512:640], si[24 * K], T.CB[:], False, True)], ["SI", "CB"], ["C1"])

        def cand_b(p):
            o = place(T.C, 0, p)
            mm(wrap(o, T.WA, T.GP, G * (2 * p + 1), p == 0, False) + [(o, si[136 * K], gone(p), False, p == 1)], ["SI", "FL", "WM"] + gp(1, p), ["C0"])

        def b_changes():
            ts(T.CB[:], T.C[:, 0:128], float(K), ALU.is_ge, w=["CB"], x=["C0"])

        def ahead(arr, p):
            if arr:
                return T.C[:, 0:128], "C0"
            if last:
                return T.STG[:, 512:640], "STG1"
            return (T.STG[:, 0:64], "STG0") if p == f else (T.STG[:, 512:576], "STG1")

        def cand_a(p):
            o, key = ahead(0, p)
            mm(wrap(place(T.STG, 512, p) if last else o, T.WA, T.GP, G * 2 * p, not (last and p), p or not last), ["WM"] + gp(0, p), [key])

        def best():
            tt(T.M[:], T.C[:, 512:768], mine[:], ALU.max, r=mkey, w=["M"], x=["C1"])

        def choose(arr, p=None):
            o, key = ahead(arr, p)
            tt(piece(T.TG, arr, p), o, piece(T.M, arr, p), ALU.max, r=["M"], w=keys("TG", arr, p), x=[key])

        def strip(arr, p=None):
            ts(piece(T.AB, arr, p), piece(T.TG, arr, p), K - 1, ALU.bitwise_and, r=keys("TG", arr, p), w=keys("AB", arr, p))

        def offsets(arr, p=None):
            cp(piece(T.OFF, arr, p), piece(T.AB, arr, p), r=keys("AB", arr, p), w=keys("OFF", arr, p))

        def floats(arr, p=None):
            op("g", g.affine_select, (piece(T.ABF, arr, p), piece(T.AB, arr, p), [[0, 64 * len(both(p))]], ALU.is_ge, 0.0, 0, 0),
               r=keys("AB", arr, p), w=keys("ABF", arr, p))

        def result(arr):
            cp(piece(T.TF, arr), piece(T.AB, arr), r=keys("AB", arr), w=["TF%d" % arr])
            dma("sa"[arr], (T.ya, T.yb)[arr][:], piece(T.TF, arr), "dy", r=["TF%d" % arr])

        def ghost_open(k):
            mm([(bank("GH%d" % k), T.IF[:], T.W[:, V + 512 * k:V + 512 * (k + 1)], True, False)], ["IF", gk[k]], ["GH%d" % k])

        def ghost_add(k):
            mm([(bank("GH%d" % k), T.IB[:], T["L%d" % (t + 1)][:, 512 * k:512 * (k + 1)], k not in OPEN, True)],
               ["IB", "L%d_%d" % (t + 1, k)], ["GH%d" % k])

        def ghost_out(k):
            o = T.W[:, V + 512 * k:V + 512 * (k + 1)]
            if k in OPEN:
                act(o, bank("GH%d" % k), ACT.Copy, w=[gk[k]], x=["GH%d" % k])
            else:
                tt(o, bank("GH%d" % k), o, ALU.add, r=[gk[k]], w=[gk[k]], x=["GH%d" % k])

        def send_moves(k):
            cols, key = slice(512 * k, 512 * (k + 1)), "S%d%d" % (t, k)
            act(T["S%d" % (t + 1)][:, cols], T.D[:].indirect(T.SN[:, 32 * k:32 * (k + 1)]), ACT.Copy, r=["D0", "D1", "SN"], w=[key])
            send(1 + k // 2, T["L%d" % (t + 1)][:, cols], T["S%d" % (t + 1)][:, cols], "ar%d_%d" % (t + 1, k), [key])

        def turn_in(s):
            for b in range(4):
                ts(T.E1[:, b:8:4, 16 * s:16 * s + 16], T.ABF[:, 128 + b::4], upper[s], ALU.mult, r=keys("ABF", 1), w=["E1%d" % s])

        def turn():
            op("v", g.vector.transpose, (T.E2[:, 0:8], T.E1[:, 0:8]), r=["E10", "E11"], w=["E2"])

        def turn_back():
            for p in range(2):
                tt(T.ABT[:, 128 + p::2], T.E2[:, 4 * p:4 * p + 4, 0:16], T.E2[:, 4 * p:4 * p + 4, 16:32], ALU.add, r=["E2"], w=["ABT1"])

        if t == 0:
            lay_ghosts();high(0);pieces(0);evac("GH0", 0, 0, 1);evac("GH1", 1, 0, 1);zed(0);evac("GH2", 0, 1, 1);evac("GH3", 1, 1, 1);lay_others();lay_turn();swap_open();lead();ghost_open(0);ghost_open(2);gap(t, pi)
        elif not last:
            ghost_open(0);lead();high(0, pa);lay_others();pieces(0, pa);ghost_open(2);zed(0, pa);swap_open();lay_turn()
        if not last:
            gap(t, pa);clip(pi);clip(pa);send_moves(1);send_moves(3);passing(t, pa);pass_votes();send_moves(0);changing(0);stage(0);send_moves(2);changing(1);turn_out(0);passing(t, pi);own_votes(pa);turn_out(1);look("a", 1, 0);want_votes();look("a", 0, f);stage(1);stage(2);move(0);own_votes(pi);ghost_add(1);look("v", 1, 1);flags();move(1);stage(3);move(2);cand_b(0);move(3);cand_b(1);look("v", 0, 1 - f, 0, SPLIT);ghost_add(3);cand_a(f);b_changes();swap_flags();swap_close();look("a", 0, 1 - f, SPLIT, 64);second(2);ghost_add(0);ghost_out(0);ghost_out(1);cand_a(1 - f);ghost_add(2);ghost_out(2);second(3);ghost_out(3);best();choose(0, f);choose(1);choose(0, 1 - f);strip(0, f);floats(0, f);strip(1);strip(0, 1 - f);offsets(0, f)
        if t < ST - 2:
            high(0, f);pieces(0, f);offsets(1);zed(0, f);floats(1);offsets(0, 1 - f);gap(t + 1, f, 0, 32);floats(0, 1 - f);gap(t + 1, f, 32, 64)
        if t == ST - 2:
            offsets(1);floats(0, 1 - f);offsets(0, 1 - f);floats(1)
        if last:
            high(0);passing(t, pa, 32, 64);lead(0);pieces(0);zed(0);lead(1);turn_in(1);lay("GH", pi, 0, True, True);evac("GH0", 0, pi);lay("STG", pa, 0, True, False);turn_in(0);passing(t, pa, 0, 32);pass_votes();evac("GH1", 1, pi);changing(0);turn_out(0);turn();changing(1);own_votes(pa);want_votes();turn_out(1);turned();turn_back();passing(t, pi);look("a", 1, 0);own_votes(pi);gap(t, 0);turned_out();gap(t, 1);swap_open();flags();clip(0);look("a", 1, 1);cand_b(0);cand_b(1);clip(1);look("v", 0, 1, 0, SPLITL);stage(0);move(0);stage(1);move(1);b_changes();stage(2);stage(3);move(3);move(2);look("a", 0, 0);look("a", 0, 1, SPLITL, 64);cand_a(0);swap_flags();swap_close();best();cand_a(1);choose(0);choose(1);strip(0);strip(1);result(1);result(0)
        continue
        if t == 0:
            high(0);pieces(0);zed(0);lay_others();lay_turn();swap_open();lead();ghost_open(0);ghost_open(2);gap(t, pi)
        elif not last:
            lead();high(0, pa);ghost_open(0);ghost_open(2);lay_others();swap_open();pieces(0, pa);zed(0, pa);lay_turn()
        if not last:
            gap(t, pa);clip(pi);clip(pa);send_moves(0);send_moves(2);send_moves(1);send_moves(3);passing(t, pa);pass_votes();changing(0);turn_out(0);stage(0);changing(1);turn_out(1);own_votes(pa);want_votes();look("a", 1, 0);stage(1);passing(t, pi);look("a", 0, f);own_votes(pi);move(0);look("v", 1, 1);stage(2);flags();move(1);move(2);cand_b(0);cand_b(1);stage(3);look("a", 0, 1 - f, SPLIT, 64);ghost_add(0);b_changes();swap_flags();swap_close();cand_a(f);ghost_add(2);move(3);best();look("v", 0, 1 - f, 0, SPLIT);choose(0, f);choose(1);strip(0, f);ghost_out(0);ghost_out(2);ghost_add(1);floats(0, f);cand_a(1 - f);ghost_out(1);choose(0, 1 - f);offsets(0, f);high(0, f);ghost_add(3);pieces(0, f);zed(0, f);strip(1);strip(0, 1 - f);ghost_out(3)
        if t < ST - 2:
            offsets(1);offsets(0, 1 - f);floats(1);floats(0, 1 - f);gap(t + 1, f, 0, 32);gap(t + 1, f, 32, 64)
        if t == ST - 2:
            offsets(1);offsets(0, 1 - f);floats(0, 1 - f);floats(1)
        if last:
            high(0, pa);passing(t, pa);lead(0);turn_in(1);lead(1);lay("GH", pi, 0, True, True);pieces(0, pa);zed(0, pa);turn_in(0);lay("STG", pa, 0, True, False);pass_votes();evac("GH0", 0, pi);evac("GH1", 1, pi);changing(0);changing(1);turn_out(0);turn();gap(t, 0);own_votes(pa);want_votes();turn_out(1);passing(t, pi);turned();look("a", 1, 0);own_votes(pi);turned_out();turn_back();swap_open();gap(t, 1);flags();cand_b(0);look("a", 1, 1);clip(0);clip(1);cand_b(1);look("v", 0, 1, 0, SPLITL);stage(0);stage(2);stage(1);stage(3);b_changes();look("a", 0, 0);look("a", 0, 1, SPLITL, 64);swap_flags();move(0);swap_close();move(2);cand_a(0);move(1);best();choose(1);cand_a(1);move(3);strip(1);choose(0);result(1);strip(0);result(0)
        continue
        if t == 0:
            high(0)
            pieces(0)
            zed(0)
            lay_others()
            lay_turn()
            swap_open()
            lead()
            ghost_open(OPEN[0])
            ghost_open(OPEN[1])
            gap(t, pi)
        elif not last:
            high(0, pa)
            lay_others()
            pieces(0, pa)
            lead()
            zed(0, pa)
            swap_open()
            ghost_open(OPEN[0])
            lay_turn()
            ghost_open(OPEN[1])
        if not last:
            f = pi if t == ST - 2 else pa
            gap(t, pa)
            clip(pi)
            clip(pa)
            send_moves(1)
            send_moves(2)
            stage(0)
            stage(1)
            passing(t, pa)
            pass_votes()
            changing()
            own_votes(pa)
            want_votes()
            passing(t, pi)
            own_votes(pi)
            move(0)
            look("a", 1, 0)
            look("v", 1, 1)
            look("a", 0, f)
            stage(2)
            flags()
            move(1)
            move(2)
            cand_b(0)
            cand_b(1)
            stage(3)
            swap_flags()
            b_changes()
            move(3)
            look("v", 0, 1 - f, 0, SPLIT)
            look("a", 0, 1 - f, SPLIT, 64)
            cand_a(f)
            swap_close()
            ghost_add(0)
            ghost_add(1)
            cand_a(1 - f)
            best()
            ghost_out(0)
            ghost_out(1)
            choose(0, f)
            choose(1)
            ghost_add(2)
            ghost_add(3)
            strip(0, f)
            strip(1)
            choose(0, 1 - f)
            floats(0, f)
            high(0, f)
            pieces(0, f)
            offsets(0, f)
            ghost_out(2)
            ghost_out(3)
            zed(0, f)
            strip(0, 1 - f)
            if t < ST - 2:
                floats(1)
                gap(t + 1, f, 0, 32)
                offsets(0, 1 - f)
                floats(0, 1 - f)
                gap(t + 1, f, 32, 64)
                offsets(1)
            else:
                floats(1)
                offsets(1)
                high(1)
                pieces(1)
                floats(0, 1 - f)
                offsets(0, 1 - f)
                passing(t + 1, f)
        else:
            lead()
            zed(1)
            high(0, pi)
            lay_turn_first = [spread("STG%d" % h, pa, h, True, False) for h in range(2)]
            pieces(0, pi)
            zed(0, pi)
            for h in range(2):
                spread("STG%d" % h, pa, h, False, False, 1)
            pass_votes()
            changing()
            for h in range(2):
                spread(others[h], pi, h, True, False, 1)
            lay_others()
            passing(t, pi)
            own_votes(pa)
            want_votes()
            own_votes(pi)
            turned()
            look("a", 1, 0)
            look("a", 1, 1)
            turned_out()
            look("a", 0, 0)
            gap(t, 0)
            gap(t, 1)
            flags()
            clip(0)
            clip(1)
            cand_b(0)
            cand_b(1)
            stage(0)
            stage(1)
            swap_open()
            stage(2)
            stage(3)
            swap_flags()
            move(0)
            b_changes()
            cand_a(0)
            swap_close()
            move(1)
            move(2)
            move(3)
            look("v", 0, 1, 0, SPLITL)
            look("a", 0, 1, SPLITL, 64)
            cand_a(1)
            best()
            choose(1)
            strip(1)
            choose(0)
            result(1)
            strip(0)
            result(0)

    for e in cnt:
        wait("g", ("c" + e, cnt[e]))
    for s in total:
        wait("g", (s, total[s]))
